import numpy as np
import ml_dtypes


def mxq(x, axis, fmt="e4m3"):
    dtype, down = {"e4m3": (ml_dtypes.float8_e4m3fn, 7), "e5m2": (ml_dtypes.float8_e5m2, 14)}[fmt]
    v = np.moveaxis(np.asarray(x, np.float32).astype(ml_dtypes.bfloat16).astype(np.float64), axis, -1)
    blocks = v.reshape(v.shape[:-1] + (-1, 32))
    amax = np.abs(blocks).max(-1, keepdims=True)
    byte = np.maximum(np.where(amax > 0, np.frexp(amax)[1] - 1 + 127, 0) - down, 1)
    scale = np.exp2(byte - 127.0)
    codes = (blocks / scale).astype(np.float32).astype(dtype).astype(np.float64)
    return np.moveaxis((codes * scale).reshape(v.shape), -1, axis)


WIDE = False


def mx_kscale(k):
    if not WIDE:
        return np.ones(k)
    levels = np.array([10, -10, 5, -5, 0])
    if k % 512:
        return np.exp2(np.random.permutation(np.resize(levels, k // 32))).repeat(32)
    a = np.empty((k // 512, 16))
    for p in range(k // 512):
        a[p, :8] = np.random.permutation(np.resize(levels, 8))
        for g in range(8):
            far = levels[np.abs(levels - a[p, g]) >= 10]
            a[p, g + 8] = far[np.random.randint(len(far))]
    return np.exp2(a.ravel()).repeat(32)


def f64(x):
    return np.asarray(x).astype(np.float64)


def striped(idx):
    return np.tile(np.asarray(idx).reshape(-1, 16).T, (8, 1)).astype(np.uint16)


def unstriped(offs):
    return offs[:16].T.reshape(-1).astype(np.int64)


E2M1 = np.array([0.0, 0.5, 1.0, 1.5, 2.0, 3.0, 4.0, 6.0, -0.0, -0.5, -1.0, -1.5, -2.0, -3.0, -4.0, -6.0])


def pack_weight(w, fmt):
    k, n = w.shape
    w = f64(np.asarray(w, np.float32).astype(ml_dtypes.bfloat16)).reshape(k // 32, 32, n)
    amax = np.abs(w).max(1)
    if fmt == "e4m3":
        byte = np.frexp(amax)[1] - 1 + 127 - 7
    else:
        mant, ex = np.frexp(amax / 6.0)
        byte = np.where(mant > 0.5, ex, ex - 1) + 127
    byte = np.clip(np.where(amax > 0, byte, 1), 1, 254)
    scaled = (w * np.exp2(127.0 - byte)[:, None, :]).reshape(k, n).astype(np.float32)
    by_word = np.ascontiguousarray(scaled.reshape(k // 512, 128, 4, n).transpose(0, 1, 3, 2))
    if fmt == "e4m3":
        words = by_word.astype(ml_dtypes.float8_e4m3fn).view(np.uint8)
    else:
        c = by_word.astype(ml_dtypes.float4_e2m1fn).view(np.uint8) & 0xF
        words = (c[..., 0::2] | (c[..., 1::2] << 4)).reshape(k // 512, 128, 2 * n)
    return np.ascontiguousarray(words), np.ascontiguousarray(byte.astype(np.uint8).reshape(k // 512, 16, n))


def unpack_weight(words, scales, fmt):
    g, _, n = scales.shape
    words = np.ascontiguousarray(words).reshape(g, 128, n, -1)
    if fmt == "e4m3":
        vals = words.view(ml_dtypes.float8_e4m3fn).astype(np.float64)
    else:
        nib = np.empty((g, 128, n, 4), np.uint8)
        nib[..., 0::2] = words & 0xF
        nib[..., 1::2] = words >> 4
        vals = E2M1[nib]
    vals = vals * np.repeat(np.exp2(scales.astype(np.float64) - 127.0), 8, axis=1)[..., None]
    return vals.transpose(0, 1, 3, 2).reshape(g * 512, n)


def bf(x):
    return np.asarray(x, np.float32).astype(ml_dtypes.bfloat16)


def planes(Y):
    r, m = Y.shape
    b = f64(bf(Y)).reshape(r // 32, 32, m)
    amax = np.abs(b).max(1)
    byte = np.clip(np.where(amax > 0, np.frexp(amax)[1] - 1 + 127 - 7, 1), 1, 254)
    codes = (b * np.exp2(127.0 - byte)[:, None, :]).reshape(r, m).astype(np.float32).astype(ml_dtypes.float8_e4m3fn).view(np.uint8)
    words = codes.reshape(r // 512, 128, 4, m).transpose(0, 1, 3, 2)
    return np.ascontiguousarray(words), np.ascontiguousarray(byte.astype(np.uint8).reshape(r // 512, 16, m))


D, T, I, M, E = 512, 2048, 512, 512, 512


def setup_inputs():
    n = np.random.standard_normal
    idx = np.random.permutation(T)[:I]
    fd = mx_kscale(D)
    fm = mx_kscale(M)
    tokp = pack_weight(n((D, T)) / fd[:, None], "e4m3")
    return {
        "tok_words": tokp[0],
        "tok_scales": tokp[1],
        "mk": (n((D, M)) * 0.5 / np.sqrt(D) * fd[:, None]).astype(np.float32),
        "msc": (np.random.uniform(8.0, 24.0, (M, 1)) * fm[:, None]).astype(np.float32),
        "mv": (n((M, E)) / fm[:, None]).astype(np.float32),
        "offs": striped(idx),
    }


def reference(tok_words, tok_scales, mk, msc, mv, offs):
    idx = unstriped(offs)
    toku = unpack_weight(tok_words, tok_scales, "e4m3")
    mkq = mxq(f64(mk), 0, "e4m3")
    tokidxg = toku[:, idx]
    a = mkq.T @ tokidxg
    p = np.exp(a - np.max(a, axis=1, keepdims=True))
    s = p / np.sum(p, axis=1, keepdims=True)
    st = s.T
    x = st / np.sum(st, axis=1, keepdims=True)
    xt = x.T
    w = xt * f64(msc)
    mvq = mxq(f64(mv), 0, "e4m3")
    wq = mxq(w, 0, "e4m3")
    y = mvq.T @ wq
    words, scales = planes(y)
    return y, words, scales

@@ -1,0 +1,220 @@
+from contextlib import ExitStack
+
+import concourse.mybir as mybir
+from concourse.masks import make_identity
+
+F32 = mybir.dt.float32
+BF16 = mybir.dt.bfloat16
+I32 = mybir.dt.int32
+U32 = mybir.dt.uint32
+U16 = mybir.dt.uint16
+U8 = mybir.dt.uint8
+FP8X4 = mybir.dt.float8_e4m3fn_x4
+ACT = mybir.ActivationFunctionType
+ALU = mybir.AluOpType
+AX = mybir.AxisListType
+
+P = 128
+PACK = 4
+D, T, I, M, E = 512, 2048, 512, 512, 512
+CHUNK = 128
+FLOPS = 2 * D * M * I + 2 * M * E * I
+
+
+def deal(copy, grouped, raw):
+    copy(out=grouped.rearrange("p t s j -> p s j t"), in_=raw.rearrange("p j (s t) -> p s j t", t=PACK))
+
+
+def tile_attend_externalattn_pl_kernel(tc, tok_words, tok_scales, mk, msc, mv, offs, out_0, out_1, out_2):
+    nc = tc.nc
+    with ExitStack() as ctx:
+        keep = ctx.enter_context(tc.tile_pool(name="keep", bufs=1))
+        psum = ctx.enter_context(tc.psum_pool(name="psum", bufs=1))
+
+        offsets = keep.tile([P, I // 16], U16, name="offsets")
+        mk_raw = [keep.tile([P, 2, M], F32, name=f"mk_raw{h}", tag=f"raw{h}", align_bytes=64) for h in range(2)]
+        pool_scales = keep.tile([P, T], U8, name="pool_scales", tag="scales_then_codes", align_bytes=64)
+
+        nc.vector.memset(pool_scales[:].bitcast(I32), 0)
+        for h in range(2):
+            nc.sync.dma_start(out=mk_raw[h][:], in_=mk.rearrange("(p j) m -> p j m", j=PACK)[:, 2 * h : 2 * h + 2, :])
+        nc.sync.dma_start(offsets[:], offs)
+        for q in range(4):
+            nc.sync.dma_start(
+                out=pool_scales[32 * q : 32 * q + 4, :].bitcast(I32),
+                in_=tok_scales[0][4 * q : 4 * q + 4, :].bitcast(I32),
+            )
+        warm = keep.tile([P, 1], F32, name="warm", tag="ones_then_words", align_bytes=64)
+        nc.gpsimd.memset(warm[:], 0.0)
+        nc.scalar.activation(out=warm[:], in_=warm[:], func=ACT.Exp)
+        ident = keep.tile([P, P], F32, name="ident")
+        make_identity(nc, ident[:])
+        pool_words = keep.tile([P, T], I32, name="pool_words", tag="ones_then_words", align_bytes=64)
+        nc.sync.dma_start(out=pool_words[:], in_=tok_words[0].rearrange("p n t -> p (n t)").bitcast(I32))
+
+
+        tok_sc = keep.tile([P, I], U8, name="tok_sc", align_bytes=64)
+        nc.vector.tensor_copy(out=tok_sc[:], in_=pool_scales[:].indirect(offsets[:]))
+
+        mk_b = keep.tile([P, PACK, P, PACK], BF16, name="mk_b", tag="rounded_then_codes", align_bytes=64)
+        deal(nc.scalar.copy, mk_b[:, :, :, 0:2], mk_raw[0][:])
+        deal(nc.vector.tensor_copy, mk_b[:, :, 0:48, 2:4], mk_raw[1][:, :, 0:192])
+        deal(nc.scalar.copy, mk_b[:, :, 48:128, 2:4], mk_raw[1][:, :, 192:512])
+        mv_raw = [keep.tile([P, PACK, E // 2], F32, name=f"mv_raw{h}", tag=f"raw{h}", align_bytes=64) for h in range(2)]
+        for h in range(2):
+            nc.sync.dma_start(out=mv_raw[h][:], in_=mv.rearrange("(p j) e -> p j e", j=PACK)[:, :, 256 * h : 256 * (h + 1)])
+        mk_codes = keep.tile([P, M], U32, name="mk_codes", tag="scales_then_codes", align_bytes=64)
+        mk_sc = keep.tile([P, M], U8, name="mk_sc", align_bytes=64)
+        nc.vector.quantize_mx(out=mk_codes[:].bitcast(FP8X4), scales=mk_sc[:], in_=mk_b[:].rearrange("p t s j -> p (t s j)"))
+
+        tok_codes = keep.tile([P, I], U32, name="tok_codes", tag="rounded_then_codes", align_bytes=64)
+        for h in range(2):
+            nc.vector.tensor_copy(
+                out=tok_codes[:, 256 * h : 256 * (h + 1)],
+                in_=pool_words[:].bitcast(U32).indirect(offsets[:, 16 * h : 16 * (h + 1)]),
+            )
+
+        msc_cols = keep.tile([P, PACK], F32, name="msc_cols", tag="ones_then_words", align_bytes=64)
+        nc.sync.dma_start(out=msc_cols[:], in_=msc.rearrange("(p t) o -> p (t o)", t=PACK))
+        mv_b0 = keep.tile([P, PACK, P // 2, PACK], BF16, name="mv_b0", align_bytes=64)
+        deal(nc.scalar.copy, mv_b0[:], mv_raw[0][:])
+
+        scores = [psum.tile([P, I], F32, name=f"scores{t}", tag=f"a{t}") for t in range(PACK)]
+        sums = [psum.tile([P, P], F32, name=f"sums{j}", tag=f"b{j}") for j in range(4)]
+        for t in range(PACK):
+            cols = slice(P * t, P * (t + 1))
+            for h in range(2):
+                slots = slice(256 * h, 256 * (h + 1))
+                nc.tensor.matmul_mx(
+                    out=scores[t][:, slots],
+                    lhsT=mk_codes[:, cols].bitcast(FP8X4),
+                    lhsT_scale=mk_sc[:, cols],
+                    rhs=tok_codes[:, slots].bitcast(FP8X4),
+                    rhs_scale=tok_sc[:, slots],
+                    start=True,
+                    stop=True,
+                )
+        p_all = keep.tile([P, PACK * I], F32, name="p_all", tag="raw0", align_bytes=64)
+        p = [p_all[:, I * t : I * (t + 1)] for t in range(PACK)]
+        s = [keep.tile([P, I], F32, name=f"s{t}", tag=f"s{t}", align_bytes=64) for t in range(PACK)]
+        neg_max = [keep.tile([P, 1], F32, name=f"neg_max{t}") for t in range(PACK)]
+        row_sum = [keep.tile([P, 1], F32, name=f"row_sum{t}", tag=f"row_sum{t}", align_bytes=64) for t in range(PACK)]
+        row_inv = [keep.tile([P, 1], F32, name=f"row_inv{t}") for t in range(PACK)]
+        sm = keep.tile([P, PACK, I], F32, name="sm")
+        for t in range(PACK):
+            nc.vector.tensor_reduce(out=neg_max[t][:], in_=scores[t][:], axis=AX.X, op=ALU.max, negate=True)
+            nc.scalar.activation(out=p[t], in_=scores[t][:], func=ACT.Exp, bias=neg_max[t][:], scale=1.0, accum_out=row_sum[t][:])
+        for t in range(PACK):
+            nc.vector.reciprocal(out=row_inv[t][:], in_=row_sum[t][:])
+            for part in ([slice(0, I)] if t < PACK - 1 else [slice(0, I // 2), slice(I // 2, I)]):
+                nc.vector.tensor_scalar(out=s[t][:, part], in0=p[t][:, part], scalar1=row_inv[t][:], scalar2=None, op0=ALU.mult)
+            for j in range(4):
+                nc.tensor.matmul(
+                    out=sums[j][:],
+                    lhsT=s[t][:, P * j : P * (j + 1)],
+                    rhs=ident[:],
+                    start=(t == 0),
+                    stop=(t == PACK - 1),
+                    is_transpose=True,
+                )
+        for t in range(PACK):
+            nc.scalar.activation(out=sm[:, t, :], in_=s[t][:], func=ACT.Copy, scale=msc_cols[:, t : t + 1])
+
+        groups = [[0], [1, 2, 3]]
+        col_sum = [keep.tile([P, len(g)], F32, name=f"col_sum{h}") for h, g in enumerate(groups)]
+        col_inv = [keep.tile([P, len(g)], F32, name=f"col_inv{h}") for h, g in enumerate(groups)]
+        spread = []
+        for h, g in enumerate(groups):
+            for u, j in enumerate(g):
+                nc.vector.tensor_reduce(out=col_sum[h][:, u : u + 1], in_=sums[j][:], axis=AX.X, op=ALU.add)
+            nc.vector.reciprocal(out=col_inv[h][:], in_=col_sum[h][:])
+            bank = psum.tile([P, len(g) * P], F32, name=f"spread{h}", tag=f"a{h}")
+            for u in range(len(g)):
+                nc.tensor.transpose(bank[:, P * u : P * (u + 1)], col_inv[h][:, u : u + 1].to_broadcast([P, P]), ident[:])
+                spread.append(bank[:, P * u : P * (u + 1)])
+
+        mv_b1 = keep.tile([P, PACK, P // 2, PACK], BF16, name="mv_b1", tag="s3", align_bytes=64)
+        mv_codes = keep.tile([P, E], U32, name="mv_codes", tag="raw0", align_bytes=64)
+        mv_sc = keep.tile([P, E], U8, name="mv_sc", align_bytes=64)
+        deal(nc.scalar.copy, mv_b1[:], mv_raw[1][:])
+        for h, mv_b in enumerate((mv_b0, mv_b1)):
+            for t in range(PACK):
+                cols = slice(P * t + 64 * h, P * t + 64 * (h + 1))
+                nc.vector.quantize_mx(out=mv_codes[:, cols].bitcast(FP8X4), scales=mv_sc[:, cols], in_=mv_b[:, t].rearrange("p s j -> p (s j)"))
+
+        y_codes = keep.tile([P, I], U32, name="y_codes", align_bytes=64)
+        y_sc = keep.tile([P, I], U8, name="y_sc", align_bytes=64)
+        out_rows = out_0.rearrange("(p t) i -> p t i", t=PACK)
+        out_words = out_1[0].rearrange("p n t -> p (n t)").bitcast(I32)
+        y_tags = ["a2", "a3", "b0", "b1"]
+        w_b = [keep.tile([P, CHUNK, PACK], BF16, name=f"w_b{j}", align_bytes=64) for j in range(4)]
+        w_codes = [keep.tile([P, CHUNK], U32, name=f"w_codes{j}", align_bytes=64) for j in range(4)]
+        w_sc = [keep.tile([P, CHUNK], U8, name=f"w_sc{j}", align_bytes=64) for j in range(4)]
+        y_sb = [keep.tile([P, PACK, CHUNK], F32, name=f"y_sb{j}") for j in range(4)]
+        y_b = [keep.tile([P, CHUNK, PACK], BF16, name=f"y_b{j}", align_bytes=64) for j in range(4)]
+
+        def weigh(j):
+            cols = slice(CHUNK * j, CHUNK * (j + 1))
+            inv = spread[j]
+            nc.vector.tensor_tensor(
+                out=w_b[j][:].rearrange("p (c n) t -> p c t n", n=4),
+                in0=sm[:, :, cols].rearrange("p t (c n) -> p c t n", n=4),
+                in1=inv.rearrange("p (c n) -> p c n", n=4).unsqueeze(2).to_broadcast([P, CHUNK // 4, PACK, 4]),
+                op=ALU.mult,
+            )
+
+        def multiply(j):
+            nc.vector.quantize_mx(out=w_codes[j][:].bitcast(FP8X4), scales=w_sc[j][:], in_=w_b[j][:].rearrange("p n t -> p (n t)"))
+            if j < 3:
+                whole = psum.tile([P, PACK, CHUNK], F32, name=f"y{j}", tag=y_tags[j])
+                banks = [whole[:, 0:2], whole[:, 2:4]]
+            else:
+                banks = [psum.tile([P, 2, CHUNK], F32, name=f"y{j}_{u}", tag=f"b{1 + u}")[:] for u in range(2)]
+            for t in range(PACK):
+                cols = slice(P * t, P * (t + 1))
+                nc.tensor.matmul_mx(
+                    out=banks[t // 2][:, t % 2, :],
+                    lhsT=mv_codes[:, cols].bitcast(FP8X4),
+                    lhsT_scale=mv_sc[:, cols],
+                    rhs=w_codes[j][:].bitcast(FP8X4),
+                    rhs_scale=w_sc[j][:],
+                    start=True,
+                    stop=True,
+                )
+            if j < 3:
+                nc.scalar.copy(out=y_sb[j][:], in_=whole[:])
+                if j == 0:
+                    nc.scalar.copy(out=y_b[j][:], in_=whole[:].rearrange("p t n -> p n t"))
+            else:
+                for u in range(2):
+                    nc.vector.tensor_copy(
+                        out=y_b[j][:, :, 2 * u : 2 * u + 2],
+                        in_=banks[u].rearrange("p t n -> p n t"),
+                    )
+                    nc.scalar.copy(out=y_sb[j][:, 2 * u : 2 * u + 2], in_=banks[u])
+            nc.sync.dma_start(out=out_rows[:, :, CHUNK * j : CHUNK * (j + 1)], in_=y_sb[j][:])
+
+        def regroup(j):
+            nc.vector.tensor_copy(
+                out=y_b[j][:].rearrange("p (c n) t -> p c t n", n=4),
+                in_=y_sb[j][:].rearrange("p t (c n) -> p c t n", n=4),
+            )
+
+        def hand_on(j):
+            cols = slice(CHUNK * j, CHUNK * (j + 1))
+            nc.vector.quantize_mx(out=y_codes[:, cols].bitcast(FP8X4), scales=y_sc[:, cols], in_=y_b[j][:].rearrange("p n t -> p (n t)"))
+            nc.sync.dma_start(out=out_words[:, cols], in_=y_codes[:, cols].bitcast(I32))
+
+        weigh(0)
+        for j in range(1, 4):
+            weigh(j)
+            multiply(j - 1)
+        multiply(3)
+        for j in range(1, 3):
+            regroup(j)
+            hand_on(j - 1)
+        hand_on(2)
+        hand_on(3)
+        for q in range(4):
+            queue = nc.sync if q % 2 == 0 else nc.scalar
+            queue.dma_start(out=out_2[0][4 * q : 4 * q + 4, :].bitcast(I32), in_=y_sc[32 * q : 32 * q + 4, :].bitcast(I32))

@@ -39,11 +39,8 @@ def tile_attend_externalattn_pl_kernel(tc, tok_words, tok_scales, mk, msc, mv, o
         for h in range(2):
             nc.sync.dma_start(out=mk_raw[h][:], in_=mk.rearrange("(p j) m -> p j m", j=PACK)[:, 2 * h : 2 * h + 2, :])
         nc.sync.dma_start(offsets[:], offs)
-        for q in range(4):
-            nc.sync.dma_start(
-                out=pool_scales[32 * q : 32 * q + 4, :].bitcast(I32),
-                in_=tok_scales[0][4 * q : 4 * q + 4, :].bitcast(I32),
-            )
+        for r in range(4):
+            nc.sync.dma_start(out=pool_scales[r:P:32, :].bitcast(I32), in_=tok_scales[0][r:16:4, :].bitcast(I32))
         warm = keep.tile([P, 1], F32, name="warm", tag="ones_then_words", align_bytes=64)
         nc.gpsimd.memset(warm[:], 0.0)
         nc.scalar.activation(out=warm[:], in_=warm[:], func=ACT.Exp)
@@ -97,10 +94,10 @@ def tile_attend_externalattn_pl_kernel(tc, tok_words, tok_scales, mk, msc, mv, o
         p_all = keep.tile([P, PACK * I], F32, name="p_all", tag="raw0", align_bytes=64)
         p = [p_all[:, I * t : I * (t + 1)] for t in range(PACK)]
         s = [keep.tile([P, I], F32, name=f"s{t}", tag=f"s{t}", align_bytes=64) for t in range(PACK)]
-        neg_max = [keep.tile([P, 1], F32, name=f"neg_max{t}") for t in range(PACK)]
+        neg_max = [keep.tile([P, 1], F32, name=f"neg_max{t}", tag=f"neg_max{t}", align_bytes=64) for t in range(PACK)]
         row_sum = [keep.tile([P, 1], F32, name=f"row_sum{t}", tag=f"row_sum{t}", align_bytes=64) for t in range(PACK)]
         row_inv = [keep.tile([P, 1], F32, name=f"row_inv{t}") for t in range(PACK)]
-        sm = keep.tile([P, PACK, I], F32, name="sm")
+        sm = keep.tile([P, PACK, I], F32, name="sm", tag="neg_max3", align_bytes=64)
         for t in range(PACK):
             nc.vector.tensor_reduce(out=neg_max[t][:], in_=scores[t][:], axis=AX.X, op=ALU.max, negate=True)
             nc.scalar.activation(out=p[t], in_=scores[t][:], func=ACT.Exp, bias=neg_max[t][:], scale=1.0, accum_out=row_sum[t][:])
@@ -136,7 +133,11 @@ def tile_attend_externalattn_pl_kernel(tc, tok_words, tok_scales, mk, msc, mv, o
         mv_b1 = keep.tile([P, PACK, P // 2, PACK], BF16, name="mv_b1", tag="s3", align_bytes=64)
         mv_codes = keep.tile([P, E], U32, name="mv_codes", tag="raw0", align_bytes=64)
         mv_sc = keep.tile([P, E], U8, name="mv_sc", align_bytes=64)
-        deal(nc.scalar.copy, mv_b1[:], mv_raw[1][:])
+        for u in range(2):
+            nc.scalar.copy(
+                out=mv_b1[:, 2 * u : 2 * u + 2].rearrange("p t s j -> p s j t"),
+                in_=mv_raw[1][:].rearrange("p j (s t) -> p s j t", t=PACK)[:, :, :, 2 * u : 2 * u + 2],
+            )
         for h, mv_b in enumerate((mv_b0, mv_b1)):
             for t in range(PACK):
                 cols = slice(P * t + 64 * h, P * t + 64 * (h + 1))
@@ -217,4 +218,4 @@ def tile_attend_externalattn_pl_kernel(tc, tok_words, tok_scales, mk, msc, mv, o
         hand_on(3)
         for q in range(4):
             queue = nc.sync if q % 2 == 0 else nc.scalar
-            queue.dma_start(out=out_2[0][4 * q : 4 * q + 4, :].bitcast(I32), in_=y_sc[32 * q : 32 * q + 4, :].bitcast(I32))
+            queue.dma_start(out=out_2[0][q:16:4, :].bitcast(I32), in_=y_sc[q:P:32, :].bitcast(I32))

@@ -97,7 +97,6 @@ def tile_attend_externalattn_pl_kernel(tc, tok_words, tok_scales, mk, msc, mv, o
         neg_max = [keep.tile([P, 1], F32, name=f"neg_max{t}", tag=f"neg_max{t}", align_bytes=64) for t in range(PACK)]
         row_sum = [keep.tile([P, 1], F32, name=f"row_sum{t}", tag=f"row_sum{t}", align_bytes=64) for t in range(PACK)]
         row_inv = [keep.tile([P, 1], F32, name=f"row_inv{t}") for t in range(PACK)]
-        sm = keep.tile([P, PACK, I], F32, name="sm", tag="neg_max3", align_bytes=64)
         for t in range(PACK):
             nc.vector.tensor_reduce(out=neg_max[t][:], in_=scores[t][:], axis=AX.X, op=ALU.max, negate=True)
             nc.scalar.activation(out=p[t], in_=scores[t][:], func=ACT.Exp, bias=neg_max[t][:], scale=1.0, accum_out=row_sum[t][:])
@@ -114,8 +113,16 @@ def tile_attend_externalattn_pl_kernel(tc, tok_words, tok_scales, mk, msc, mv, o
                     stop=(t == PACK - 1),
                     is_transpose=True,
                 )
-        for t in range(PACK):
-            nc.scalar.activation(out=sm[:, t, :], in_=s[t][:], func=ACT.Copy, scale=msc_cols[:, t : t + 1])
+        sm = []
+
+        def scale_by_key(tag):
+            h = len(sm)
+            half = keep.tile([P, PACK, I // 2], F32, name=f"sm{h}", tag=tag, align_bytes=64)
+            for t in range(PACK):
+                nc.scalar.activation(out=half[:, t, :], in_=s[t][:, 256 * h : 256 * (h + 1)], func=ACT.Copy, scale=msc_cols[:, t : t + 1])
+            sm.append(half)
+
+        scale_by_key("neg_max3")
 
         groups = [[0], [1, 2, 3]]
         col_sum = [keep.tile([P, len(g)], F32, name=f"col_sum{h}") for h, g in enumerate(groups)]
@@ -130,7 +137,7 @@ def tile_attend_externalattn_pl_kernel(tc, tok_words, tok_scales, mk, msc, mv, o
                 nc.tensor.transpose(bank[:, P * u : P * (u + 1)], col_inv[h][:, u : u + 1].to_broadcast([P, P]), ident[:])
                 spread.append(bank[:, P * u : P * (u + 1)])
 
-        mv_b1 = keep.tile([P, PACK, P // 2, PACK], BF16, name="mv_b1", tag="s3", align_bytes=64)
+        mv_b1 = keep.tile([P, PACK, P // 2, PACK], BF16, name="mv_b1", tag="row_sum3", align_bytes=64)
         mv_codes = keep.tile([P, E], U32, name="mv_codes", tag="raw0", align_bytes=64)
         mv_sc = keep.tile([P, E], U8, name="mv_sc", align_bytes=64)
         for u in range(2):
@@ -138,6 +145,7 @@ def tile_attend_externalattn_pl_kernel(tc, tok_words, tok_scales, mk, msc, mv, o
                 out=mv_b1[:, 2 * u : 2 * u + 2].rearrange("p t s j -> p s j t"),
                 in_=mv_raw[1][:].rearrange("p j (s t) -> p s j t", t=PACK)[:, :, :, 2 * u : 2 * u + 2],
             )
+        scale_by_key("raw1")
         for h, mv_b in enumerate((mv_b0, mv_b1)):
             for t in range(PACK):
                 cols = slice(P * t + 64 * h, P * t + 64 * (h + 1))
@@ -155,11 +163,11 @@ def tile_attend_externalattn_pl_kernel(tc, tok_words, tok_scales, mk, msc, mv, o
         y_b = [keep.tile([P, CHUNK, PACK], BF16, name=f"y_b{j}", align_bytes=64) for j in range(4)]
 
         def weigh(j):
-            cols = slice(CHUNK * j, CHUNK * (j + 1))
+            cols = slice(CHUNK * (j % 2), CHUNK * (j % 2 + 1))
             inv = spread[j]
             nc.vector.tensor_tensor(
                 out=w_b[j][:].rearrange("p (c n) t -> p c t n", n=4),
-                in0=sm[:, :, cols].rearrange("p t (c n) -> p c t n", n=4),
+                in0=sm[j // 2][:, :, cols].rearrange("p t (c n) -> p c t n", n=4),
                 in1=inv.rearrange("p (c n) -> p c n", n=4).unsqueeze(2).to_broadcast([P, CHUNK // 4, PACK, 4]),
                 op=ALU.mult,
             )
@@ -204,10 +212,11 @@ def tile_attend_externalattn_pl_kernel(tc, tok_words, tok_scales, mk, msc, mv, o
         def hand_on(j):
             cols = slice(CHUNK * j, CHUNK * (j + 1))
             nc.vector.quantize_mx(out=y_codes[:, cols].bitcast(FP8X4), scales=y_sc[:, cols], in_=y_b[j][:].rearrange("p n t -> p (n t)"))
-            nc.sync.dma_start(out=out_words[:, cols], in_=y_codes[:, cols].bitcast(I32))
 
         weigh(0)
-        for j in range(1, 4):
+        multiply(0)
+        weigh(1)
+        for j in range(2, 4):
             weigh(j)
             multiply(j - 1)
         multiply(3)
@@ -216,6 +225,7 @@ def tile_attend_externalattn_pl_kernel(tc, tok_words, tok_scales, mk, msc, mv, o
             hand_on(j - 1)
         hand_on(2)
         hand_on(3)
+        nc.sync.dma_start(out=out_words, in_=y_codes[:].bitcast(I32))
         for q in range(4):
             queue = nc.sync if q % 2 == 0 else nc.scalar
             queue.dma_start(out=out_2[0][q:16:4, :].bitcast(I32), in_=y_sc[q:P:32, :].bitcast(I32))

@@ -18,6 +18,7 @@ P = 128
 PACK = 4
 D, T, I, M, E = 512, 2048, 512, 512, 512
 CHUNK = 128
+MK_VECTOR_SHARE = 44
 FLOPS = 2 * D * M * I + 2 * M * E * I
 
 
@@ -32,35 +33,31 @@ def tile_attend_externalattn_pl_kernel(tc, tok_words, tok_scales, mk, msc, mv, o
         psum = ctx.enter_context(tc.psum_pool(name="psum", bufs=1))
 
         offsets = keep.tile([P, I // 16], U16, name="offsets")
-        mk_raw = [keep.tile([P, 2, M], F32, name=f"mk_raw{h}", tag=f"raw{h}", align_bytes=64) for h in range(2)]
-        pool_scales = keep.tile([P, T], U8, name="pool_scales", tag="scales_then_codes", align_bytes=64)
+        mk_raw = keep.tile([P, PACK, M], F32, name="mk_raw", align_bytes=64)
+        pool_scales = keep.tile([P, T], U8, name="pool_scales", align_bytes=64)
+        pool_words = keep.tile([P, T], I32, name="pool_words", align_bytes=64)
+        msc_cols = keep.tile([P, PACK], F32, name="msc_cols", align_bytes=64)
+        mv_raw = [keep.tile([P, PACK, E // 2], F32, name=f"mv_raw{h}", align_bytes=64) for h in range(2)]
 
-        nc.vector.memset(pool_scales[:].bitcast(I32), 0)
-        for h in range(2):
-            nc.sync.dma_start(out=mk_raw[h][:], in_=mk.rearrange("(p j) m -> p j m", j=PACK)[:, 2 * h : 2 * h + 2, :])
+        nc.gpsimd.memset(pool_scales[:].bitcast(I32), 0)
+        nc.sync.dma_start(out=mk_raw[:], in_=mk.rearrange("(p j) m -> p j m", j=PACK))
         nc.sync.dma_start(offsets[:], offs)
         for r in range(4):
             nc.sync.dma_start(out=pool_scales[r:P:32, :].bitcast(I32), in_=tok_scales[0][r:16:4, :].bitcast(I32))
-        warm = keep.tile([P, 1], F32, name="warm", tag="ones_then_words", align_bytes=64)
-        nc.gpsimd.memset(warm[:], 0.0)
-        nc.scalar.activation(out=warm[:], in_=warm[:], func=ACT.Exp)
-        ident = keep.tile([P, P], F32, name="ident")
-        make_identity(nc, ident[:])
-        pool_words = keep.tile([P, T], I32, name="pool_words", tag="ones_then_words", align_bytes=64)
         nc.sync.dma_start(out=pool_words[:], in_=tok_words[0].rearrange("p n t -> p (n t)").bitcast(I32))
-
-
-        tok_sc = keep.tile([P, I], U8, name="tok_sc", align_bytes=64)
-        nc.vector.tensor_copy(out=tok_sc[:], in_=pool_scales[:].indirect(offsets[:]))
-
-        mk_b = keep.tile([P, PACK, P, PACK], BF16, name="mk_b", tag="rounded_then_codes", align_bytes=64)
-        deal(nc.scalar.copy, mk_b[:, :, :, 0:2], mk_raw[0][:])
-        deal(nc.vector.tensor_copy, mk_b[:, :, 0:48, 2:4], mk_raw[1][:, :, 0:192])
-        deal(nc.scalar.copy, mk_b[:, :, 48:128, 2:4], mk_raw[1][:, :, 192:512])
-        mv_raw = [keep.tile([P, PACK, E // 2], F32, name=f"mv_raw{h}", tag=f"raw{h}", align_bytes=64) for h in range(2)]
+        nc.scalar.dma_start(out=msc_cols[:], in_=msc.rearrange("(p t) o -> p (t o)", t=PACK))
         for h in range(2):
             nc.sync.dma_start(out=mv_raw[h][:], in_=mv.rearrange("(p j) e -> p j e", j=PACK)[:, :, 256 * h : 256 * (h + 1)])
-        mk_codes = keep.tile([P, M], U32, name="mk_codes", tag="scales_then_codes", align_bytes=64)
+        ident = keep.tile([P, P], F32, name="ident")
+        make_identity(nc, ident[:])
+
+        mk_b = keep.tile([P, PACK, P, PACK], BF16, name="mk_b", tag="rounded_then_codes", align_bytes=64)
+        cut = MK_VECTOR_SHARE
+        deal(nc.vector.tensor_copy, mk_b[:, :, 0:cut, :], mk_raw[:, :, 0 : PACK * cut])
+        deal(nc.scalar.copy, mk_b[:, :, cut:P, :], mk_raw[:, :, PACK * cut : M])
+        tok_sc = keep.tile([P, I], U8, name="tok_sc", align_bytes=64)
+        nc.vector.tensor_copy(out=tok_sc[:], in_=pool_scales[:].indirect(offsets[:]))
+        mk_codes = keep.tile([P, M], U32, name="mk_codes", align_bytes=64)
         mk_sc = keep.tile([P, M], U8, name="mk_sc", align_bytes=64)
         nc.vector.quantize_mx(out=mk_codes[:].bitcast(FP8X4), scales=mk_sc[:], in_=mk_b[:].rearrange("p t s j -> p (t s j)"))
 
@@ -71,8 +68,6 @@ def tile_attend_externalattn_pl_kernel(tc, tok_words, tok_scales, mk, msc, mv, o
                 in_=pool_words[:].bitcast(U32).indirect(offsets[:, 16 * h : 16 * (h + 1)]),
             )
 
-        msc_cols = keep.tile([P, PACK], F32, name="msc_cols", tag="ones_then_words", align_bytes=64)
-        nc.sync.dma_start(out=msc_cols[:], in_=msc.rearrange("(p t) o -> p (t o)", t=PACK))
         mv_b0 = keep.tile([P, PACK, P // 2, PACK], BF16, name="mv_b0", align_bytes=64)
         deal(nc.scalar.copy, mv_b0[:], mv_raw[0][:])
 
@@ -91,7 +86,7 @@ def tile_attend_externalattn_pl_kernel(tc, tok_words, tok_scales, mk, msc, mv, o
                     start=True,
                     stop=True,
                 )
-        p_all = keep.tile([P, PACK * I], F32, name="p_all", tag="raw0", align_bytes=64)
+        p_all = keep.tile([P, PACK * I], F32, name="p_all", tag="mv_raw0", align_bytes=64)
         p = [p_all[:, I * t : I * (t + 1)] for t in range(PACK)]
         s = [keep.tile([P, I], F32, name=f"s{t}", tag=f"s{t}", align_bytes=64) for t in range(PACK)]
         neg_max = [keep.tile([P, 1], F32, name=f"neg_max{t}", tag=f"neg_max{t}", align_bytes=64) for t in range(PACK)]
@@ -100,6 +95,17 @@ def tile_attend_externalattn_pl_kernel(tc, tok_words, tok_scales, mk, msc, mv, o
         for t in range(PACK):
             nc.vector.tensor_reduce(out=neg_max[t][:], in_=scores[t][:], axis=AX.X, op=ALU.max, negate=True)
             nc.scalar.activation(out=p[t], in_=scores[t][:], func=ACT.Exp, bias=neg_max[t][:], scale=1.0, accum_out=row_sum[t][:])
+        idle = psum.tile([P, I], F32, name="idle", tag="a1")
+        for u in range(2):
+            nc.tensor.matmul_mx(
+                out=idle[:],
+                lhsT=mk_codes[:, 0:P].bitcast(FP8X4),
+                lhsT_scale=mk_sc[:, 0:P],
+                rhs=tok_codes[:].bitcast(FP8X4),
+                rhs_scale=tok_sc[:],
+                start=True,
+                stop=True,
+            )
         for t in range(PACK):
             nc.vector.reciprocal(out=row_inv[t][:], in_=row_sum[t][:])
             for part in ([slice(0, I)] if t < PACK - 1 else [slice(0, I // 2), slice(I // 2, I)]):
@@ -138,14 +144,14 @@ def tile_attend_externalattn_pl_kernel(tc, tok_words, tok_scales, mk, msc, mv, o
                 spread.append(bank[:, P * u : P * (u + 1)])
 
         mv_b1 = keep.tile([P, PACK, P // 2, PACK], BF16, name="mv_b1", tag="row_sum3", align_bytes=64)
-        mv_codes = keep.tile([P, E], U32, name="mv_codes", tag="raw0", align_bytes=64)
+        mv_codes = keep.tile([P, E], U32, name="mv_codes", tag="mv_raw0", align_bytes=64)
         mv_sc = keep.tile([P, E], U8, name="mv_sc", align_bytes=64)
         for u in range(2):
             nc.scalar.copy(
                 out=mv_b1[:, 2 * u : 2 * u + 2].rearrange("p t s j -> p s j t"),
                 in_=mv_raw[1][:].rearrange("p j (s t) -> p s j t", t=PACK)[:, :, :, 2 * u : 2 * u + 2],
             )
-        scale_by_key("raw1")
+        scale_by_key("mv_raw1")
         for h, mv_b in enumerate((mv_b0, mv_b1)):
             for t in range(PACK):
                 cols = slice(P * t + 64 * h, P * t + 64 * (h + 1))

@@ -72,7 +72,6 @@ def tile_attend_externalattn_pl_kernel(tc, tok_words, tok_scales, mk, msc, mv, o
         deal(nc.scalar.copy, mv_b0[:], mv_raw[0][:])
 
         scores = [psum.tile([P, I], F32, name=f"scores{t}", tag=f"a{t}") for t in range(PACK)]
-        sums = [psum.tile([P, P], F32, name=f"sums{j}", tag=f"b{j}") for j in range(4)]
         for t in range(PACK):
             cols = slice(P * t, P * (t + 1))
             for h in range(2):
@@ -90,11 +89,13 @@ def tile_attend_externalattn_pl_kernel(tc, tok_words, tok_scales, mk, msc, mv, o
         p = [p_all[:, I * t : I * (t + 1)] for t in range(PACK)]
         s = [keep.tile([P, I], F32, name=f"s{t}", tag=f"s{t}", align_bytes=64) for t in range(PACK)]
         neg_max = [keep.tile([P, 1], F32, name=f"neg_max{t}", tag=f"neg_max{t}", align_bytes=64) for t in range(PACK)]
-        row_sum = [keep.tile([P, 1], F32, name=f"row_sum{t}", tag=f"row_sum{t}", align_bytes=64) for t in range(PACK)]
-        row_inv = [keep.tile([P, 1], F32, name=f"row_inv{t}") for t in range(PACK)]
+        place = [(0, 0), (0, 1), (1, 0), (2, 0)]
+        row_sum = [keep.tile([P, n], F32, name=f"row_sum{g}", align_bytes=64) for g, n in enumerate((2, 1, 1))]
+        row_inv = [keep.tile([P, n], F32, name=f"row_inv{g}", align_bytes=64) for g, n in enumerate((2, 1, 1))]
         for t in range(PACK):
+            g, c = place[t]
             nc.vector.tensor_reduce(out=neg_max[t][:], in_=scores[t][:], axis=AX.X, op=ALU.max, negate=True)
-            nc.scalar.activation(out=p[t], in_=scores[t][:], func=ACT.Exp, bias=neg_max[t][:], scale=1.0, accum_out=row_sum[t][:])
+            nc.scalar.activation(out=p[t], in_=scores[t][:], func=ACT.Exp, bias=neg_max[t][:], scale=1.0, accum_out=row_sum[g][:, c : c + 1])
         idle = psum.tile([P, I], F32, name="idle", tag="a1")
         for u in range(2):
             nc.tensor.matmul_mx(
@@ -106,62 +107,57 @@ def tile_attend_externalattn_pl_kernel(tc, tok_words, tok_scales, mk, msc, mv, o
                 start=True,
                 stop=True,
             )
-        for t in range(PACK):
-            nc.vector.reciprocal(out=row_inv[t][:], in_=row_sum[t][:])
-            for part in ([slice(0, I)] if t < PACK - 1 else [slice(0, I // 2), slice(I // 2, I)]):
-                nc.vector.tensor_scalar(out=s[t][:, part], in0=p[t][:, part], scalar1=row_inv[t][:], scalar2=None, op0=ALU.mult)
-            for j in range(4):
-                nc.tensor.matmul(
-                    out=sums[j][:],
-                    lhsT=s[t][:, P * j : P * (j + 1)],
-                    rhs=ident[:],
-                    start=(t == 0),
-                    stop=(t == PACK - 1),
-                    is_transpose=True,
-                )
-        sm = []
-
-        def scale_by_key(tag):
-            h = len(sm)
-            half = keep.tile([P, PACK, I // 2], F32, name=f"sm{h}", tag=tag, align_bytes=64)
+        for g in range(3):
+            nc.vector.reciprocal(out=row_inv[g][:], in_=row_sum[g][:])
+        for t, part in ((0, slice(0, I)), (1, slice(0, I)), (2, slice(0, I)), (3, slice(0, I // 2)), (3, slice(I // 2, I))):
+            g, c = place[t]
+            nc.vector.tensor_scalar(out=s[t][:, part], in0=p[t][:, part], scalar1=row_inv[g][:, c : c + 1], scalar2=None, op0=ALU.mult)
+        groups = [[0], [1], [2, 3]]
+        sums = [psum.tile([P, len(g), P], F32, name=f"sums{h}", tag=f"b{h}") for h, g in enumerate(groups)]
+        for h, g in enumerate(groups):
             for t in range(PACK):
-                nc.scalar.activation(out=half[:, t, :], in_=s[t][:, 256 * h : 256 * (h + 1)], func=ACT.Copy, scale=msc_cols[:, t : t + 1])
-            sm.append(half)
-
-        scale_by_key("neg_max3")
-
-        groups = [[0], [1, 2, 3]]
+                for u, j in enumerate(g):
+                    nc.tensor.matmul(
+                        out=sums[h][:, u, :],
+                        lhsT=s[t][:, P * j : P * (j + 1)],
+                        rhs=ident[:],
+                        start=(t == 0 and u == 0),
+                        stop=(t == PACK - 1 and u == len(g) - 1),
+                        is_transpose=True,
+                    )
         col_sum = [keep.tile([P, len(g)], F32, name=f"col_sum{h}") for h, g in enumerate(groups)]
         col_inv = [keep.tile([P, len(g)], F32, name=f"col_inv{h}") for h, g in enumerate(groups)]
         spread = []
         for h, g in enumerate(groups):
-            for u, j in enumerate(g):
-                nc.vector.tensor_reduce(out=col_sum[h][:, u : u + 1], in_=sums[j][:], axis=AX.X, op=ALU.add)
+            nc.vector.tensor_reduce(out=col_sum[h][:], in_=sums[h][:], axis=AX.X, op=ALU.add)
             nc.vector.reciprocal(out=col_inv[h][:], in_=col_sum[h][:])
-            bank = psum.tile([P, len(g) * P], F32, name=f"spread{h}", tag=f"a{h}")
+            bank = psum.tile([P, len(g) * P], F32, name=f"spread{h}", tag=("a0", "a1", "a2")[h])
             for u in range(len(g)):
                 nc.tensor.transpose(bank[:, P * u : P * (u + 1)], col_inv[h][:, u : u + 1].to_broadcast([P, P]), ident[:])
                 spread.append(bank[:, P * u : P * (u + 1)])
 
-        mv_b1 = keep.tile([P, PACK, P // 2, PACK], BF16, name="mv_b1", tag="row_sum3", align_bytes=64)
+        mv_b1 = keep.tile([P, PACK, P // 2, PACK], BF16, name="mv_b1", tag="neg_max3", align_bytes=64)
+        deal(nc.scalar.copy, mv_b1[:], mv_raw[1][:])
+        spans = [slice(0, 128), slice(128, 256), slice(256, 512)]
+        parts = [keep.tile([P, PACK, c.stop - c.start], F32, name=f"sm{h}", tag=tag, align_bytes=64) for h, (c, tag) in enumerate(zip(spans, ("row_sum2", "neg_max2", "mv_raw1")))]
+        for part, c in zip(parts, spans):
+            for t in range(PACK):
+                nc.scalar.activation(out=part[:, t, :], in_=s[t][:, c], func=ACT.Copy, scale=msc_cols[:, t : t + 1])
+        sm = [parts[0][:], parts[1][:], parts[2][:, :, 0:CHUNK], parts[2][:, :, CHUNK : 2 * CHUNK]]
         mv_codes = keep.tile([P, E], U32, name="mv_codes", tag="mv_raw0", align_bytes=64)
         mv_sc = keep.tile([P, E], U8, name="mv_sc", align_bytes=64)
-        for u in range(2):
-            nc.scalar.copy(
-                out=mv_b1[:, 2 * u : 2 * u + 2].rearrange("p t s j -> p s j t"),
-                in_=mv_raw[1][:].rearrange("p j (s t) -> p s j t", t=PACK)[:, :, :, 2 * u : 2 * u + 2],
-            )
-        scale_by_key("mv_raw1")
-        for h, mv_b in enumerate((mv_b0, mv_b1)):
-            for t in range(PACK):
-                cols = slice(P * t + 64 * h, P * t + 64 * (h + 1))
-                nc.vector.quantize_mx(out=mv_codes[:, cols].bitcast(FP8X4), scales=mv_sc[:, cols], in_=mv_b[:, t].rearrange("p s j -> p (s j)"))
+
+        def quantise_mv():
+            for h, mv_b in enumerate((mv_b0, mv_b1)):
+                for t in range(PACK):
+                    cols = slice(P * t + 64 * h, P * t + 64 * (h + 1))
+                    nc.vector.quantize_mx(out=mv_codes[:, cols].bitcast(FP8X4), scales=mv_sc[:, cols], in_=mv_b[:, t].rearrange("p s j -> p (s j)"))
 
         y_codes = keep.tile([P, I], U32, name="y_codes", align_bytes=64)
         y_sc = keep.tile([P, I], U8, name="y_sc", align_bytes=64)
         out_rows = out_0.rearrange("(p t) i -> p t i", t=PACK)
         out_words = out_1[0].rearrange("p n t -> p (n t)").bitcast(I32)
-        y_tags = ["a2", "a3", "b0", "b1"]
+        y_tags = ["a3", "b3", "b0"]
         w_b = [keep.tile([P, CHUNK, PACK], BF16, name=f"w_b{j}", align_bytes=64) for j in range(4)]
         w_codes = [keep.tile([P, CHUNK], U32, name=f"w_codes{j}", align_bytes=64) for j in range(4)]
         w_sc = [keep.tile([P, CHUNK], U8, name=f"w_sc{j}", align_bytes=64) for j in range(4)]
@@ -169,11 +165,10 @@ def tile_attend_externalattn_pl_kernel(tc, tok_words, tok_scales, mk, msc, mv, o
         y_b = [keep.tile([P, CHUNK, PACK], BF16, name=f"y_b{j}", align_bytes=64) for j in range(4)]
 
         def weigh(j):
-            cols = slice(CHUNK * (j % 2), CHUNK * (j % 2 + 1))
             inv = spread[j]
             nc.vector.tensor_tensor(
                 out=w_b[j][:].rearrange("p (c n) t -> p c t n", n=4),
-                in0=sm[j // 2][:, :, cols].rearrange("p t (c n) -> p c t n", n=4),
+                in0=sm[j].rearrange("p t (c n) -> p c t n", n=4),
                 in1=inv.rearrange("p (c n) -> p c n", n=4).unsqueeze(2).to_broadcast([P, CHUNK // 4, PACK, 4]),
                 op=ALU.mult,
             )
@@ -184,7 +179,7 @@ def tile_attend_externalattn_pl_kernel(tc, tok_words, tok_scales, mk, msc, mv, o
                 whole = psum.tile([P, PACK, CHUNK], F32, name=f"y{j}", tag=y_tags[j])
                 banks = [whole[:, 0:2], whole[:, 2:4]]
             else:
-                banks = [psum.tile([P, 2, CHUNK], F32, name=f"y{j}_{u}", tag=f"b{1 + u}")[:] for u in range(2)]
+                banks = [psum.tile([P, 2, CHUNK], F32, name=f"y{j}_{u}", tag=("b1", "b2")[u])[:] for u in range(2)]
             for t in range(PACK):
                 cols = slice(P * t, P * (t + 1))
                 nc.tensor.matmul_mx(
@@ -220,9 +215,8 @@ def tile_attend_externalattn_pl_kernel(tc, tok_words, tok_scales, mk, msc, mv, o
             nc.vector.quantize_mx(out=y_codes[:, cols].bitcast(FP8X4), scales=y_sc[:, cols], in_=y_b[j][:].rearrange("p n t -> p (n t)"))
 
         weigh(0)
-        multiply(0)
-        weigh(1)
-        for j in range(2, 4):
+        quantise_mv()
+        for j in range(1, 4):
             weigh(j)
             multiply(j - 1)
         multiply(3)

@@ -96,17 +96,6 @@ def tile_attend_externalattn_pl_kernel(tc, tok_words, tok_scales, mk, msc, mv, o
             g, c = place[t]
             nc.vector.tensor_reduce(out=neg_max[t][:], in_=scores[t][:], axis=AX.X, op=ALU.max, negate=True)
             nc.scalar.activation(out=p[t], in_=scores[t][:], func=ACT.Exp, bias=neg_max[t][:], scale=1.0, accum_out=row_sum[g][:, c : c + 1])
-        idle = psum.tile([P, I], F32, name="idle", tag="a1")
-        for u in range(2):
-            nc.tensor.matmul_mx(
-                out=idle[:],
-                lhsT=mk_codes[:, 0:P].bitcast(FP8X4),
-                lhsT_scale=mk_sc[:, 0:P],
-                rhs=tok_codes[:].bitcast(FP8X4),
-                rhs_scale=tok_sc[:],
-                start=True,
-                stop=True,
-            )
         for g in range(3):
             nc.vector.reciprocal(out=row_inv[g][:], in_=row_sum[g][:])
         for t, part in ((0, slice(0, I)), (1, slice(0, I)), (2, slice(0, I)), (3, slice(0, I // 2)), (3, slice(I // 2, I))):
@@ -136,14 +125,25 @@ def tile_attend_externalattn_pl_kernel(tc, tok_words, tok_scales, mk, msc, mv, o
                 nc.tensor.transpose(bank[:, P * u : P * (u + 1)], col_inv[h][:, u : u + 1].to_broadcast([P, P]), ident[:])
                 spread.append(bank[:, P * u : P * (u + 1)])
 
+        idle = psum.tile([P, I], F32, name="idle", tag="b2")
+        for u in range(2):
+            nc.tensor.matmul_mx(
+                out=idle[:],
+                lhsT=mk_codes[:, 0:P].bitcast(FP8X4),
+                lhsT_scale=mk_sc[:, 0:P],
+                rhs=tok_codes[:].bitcast(FP8X4),
+                rhs_scale=tok_sc[:],
+                start=True,
+                stop=True,
+            )
         mv_b1 = keep.tile([P, PACK, P // 2, PACK], BF16, name="mv_b1", tag="neg_max3", align_bytes=64)
         deal(nc.scalar.copy, mv_b1[:], mv_raw[1][:])
-        spans = [slice(0, 128), slice(128, 256), slice(256, 512)]
-        parts = [keep.tile([P, PACK, c.stop - c.start], F32, name=f"sm{h}", tag=tag, align_bytes=64) for h, (c, tag) in enumerate(zip(spans, ("row_sum2", "neg_max2", "mv_raw1")))]
+        spans = [slice(CHUNK * j, CHUNK * (j + 1)) for j in range(4)]
+        parts = [keep.tile([P, PACK, c.stop - c.start], F32, name=f"sm{h}", tag=tag, align_bytes=64) for h, (c, tag) in enumerate(zip(spans, ("row_sum2", "neg_max2", "mv_raw1", "neg_max1")))]
         for part, c in zip(parts, spans):
             for t in range(PACK):
                 nc.scalar.activation(out=part[:, t, :], in_=s[t][:, c], func=ACT.Copy, scale=msc_cols[:, t : t + 1])
-        sm = [parts[0][:], parts[1][:], parts[2][:, :, 0:CHUNK], parts[2][:, :, CHUNK : 2 * CHUNK]]
+        sm = [part[:] for part in parts]
         mv_codes = keep.tile([P, E], U32, name="mv_codes", tag="mv_raw0", align_bytes=64)
         mv_sc = keep.tile([P, E], U8, name="mv_sc", align_bytes=64)
 
@@ -157,12 +157,13 @@ def tile_attend_externalattn_pl_kernel(tc, tok_words, tok_scales, mk, msc, mv, o
         y_sc = keep.tile([P, I], U8, name="y_sc", align_bytes=64)
         out_rows = out_0.rearrange("(p t) i -> p t i", t=PACK)
         out_words = out_1[0].rearrange("p n t -> p (n t)").bitcast(I32)
-        y_tags = ["a3", "b3", "b0"]
+        y_tags = ["a3", "b3", "b0", "b1"]
         w_b = [keep.tile([P, CHUNK, PACK], BF16, name=f"w_b{j}", align_bytes=64) for j in range(4)]
         w_codes = [keep.tile([P, CHUNK], U32, name=f"w_codes{j}", align_bytes=64) for j in range(4)]
         w_sc = [keep.tile([P, CHUNK], U8, name=f"w_sc{j}", align_bytes=64) for j in range(4)]
         y_sb = [keep.tile([P, PACK, CHUNK], F32, name=f"y_sb{j}") for j in range(4)]
-        y_b = [keep.tile([P, CHUNK, PACK], BF16, name=f"y_b{j}", align_bytes=64) for j in range(4)]
+        y_rounded = keep.tile([P, I, PACK], BF16, name="y_rounded", tag="w_b3", align_bytes=64)
+        y_b = [y_rounded[:, CHUNK * j : CHUNK * (j + 1), :] for j in range(4)]
 
         def weigh(j):
             inv = spread[j]
@@ -175,15 +176,11 @@ def tile_attend_externalattn_pl_kernel(tc, tok_words, tok_scales, mk, msc, mv, o
 
         def multiply(j):
             nc.vector.quantize_mx(out=w_codes[j][:].bitcast(FP8X4), scales=w_sc[j][:], in_=w_b[j][:].rearrange("p n t -> p (n t)"))
-            if j < 3:
-                whole = psum.tile([P, PACK, CHUNK], F32, name=f"y{j}", tag=y_tags[j])
-                banks = [whole[:, 0:2], whole[:, 2:4]]
-            else:
-                banks = [psum.tile([P, 2, CHUNK], F32, name=f"y{j}_{u}", tag=("b1", "b2")[u])[:] for u in range(2)]
+            bank = psum.tile([P, PACK, CHUNK], F32, name=f"y{j}", tag=y_tags[j])
             for t in range(PACK):
                 cols = slice(P * t, P * (t + 1))
                 nc.tensor.matmul_mx(
-                    out=banks[t // 2][:, t % 2, :],
+                    out=bank[:, t, :],
                     lhsT=mv_codes[:, cols].bitcast(FP8X4),
                     lhsT_scale=mv_sc[:, cols],
                     rhs=w_codes[j][:].bitcast(FP8X4),
@@ -191,28 +188,17 @@ def tile_attend_externalattn_pl_kernel(tc, tok_words, tok_scales, mk, msc, mv, o
                     start=True,
                     stop=True,
                 )
-            if j < 3:
-                nc.scalar.copy(out=y_sb[j][:], in_=whole[:])
-                if j == 0:
-                    nc.scalar.copy(out=y_b[j][:], in_=whole[:].rearrange("p t n -> p n t"))
-            else:
-                for u in range(2):
-                    nc.vector.tensor_copy(
-                        out=y_b[j][:, :, 2 * u : 2 * u + 2],
-                        in_=banks[u].rearrange("p t n -> p n t"),
-                    )
-                    nc.scalar.copy(out=y_sb[j][:, 2 * u : 2 * u + 2], in_=banks[u])
+            nc.scalar.copy(out=y_sb[j][:], in_=bank[:])
             nc.sync.dma_start(out=out_rows[:, :, CHUNK * j : CHUNK * (j + 1)], in_=y_sb[j][:])
 
         def regroup(j):
             nc.vector.tensor_copy(
-                out=y_b[j][:].rearrange("p (c n) t -> p c t n", n=4),
+                out=y_b[j].rearrange("p (c n) t -> p c t n", n=4),
                 in_=y_sb[j][:].rearrange("p t (c n) -> p c t n", n=4),
             )
 
-        def hand_on(j):
-            cols = slice(CHUNK * j, CHUNK * (j + 1))
-            nc.vector.quantize_mx(out=y_codes[:, cols].bitcast(FP8X4), scales=y_sc[:, cols], in_=y_b[j][:].rearrange("p n t -> p (n t)"))
+        def hand_on(cols):
+            nc.vector.quantize_mx(out=y_codes[:, cols].bitcast(FP8X4), scales=y_sc[:, cols], in_=y_rounded[:, cols, :].rearrange("p n t -> p (n t)"))
 
         weigh(0)
         quantise_mv()
@@ -220,11 +206,10 @@ def tile_attend_externalattn_pl_kernel(tc, tok_words, tok_scales, mk, msc, mv, o
             weigh(j)
             multiply(j - 1)
         multiply(3)
-        for j in range(1, 3):
+        for j in range(4):
             regroup(j)
-            hand_on(j - 1)
-        hand_on(2)
-        hand_on(3)
+        for cols in (slice(0, 256), slice(256, 384), slice(384, 512)):
+            hand_on(cols)
         nc.sync.dma_start(out=out_words, in_=y_codes[:].bitcast(I32))
         for q in range(4):
             queue = nc.sync if q % 2 == 0 else nc.scalar

@@ -96,6 +96,17 @@ def tile_attend_externalattn_pl_kernel(tc, tok_words, tok_scales, mk, msc, mv, o
             g, c = place[t]
             nc.vector.tensor_reduce(out=neg_max[t][:], in_=scores[t][:], axis=AX.X, op=ALU.max, negate=True)
             nc.scalar.activation(out=p[t], in_=scores[t][:], func=ACT.Exp, bias=neg_max[t][:], scale=1.0, accum_out=row_sum[g][:, c : c + 1])
+        idle = psum.tile([P, I], F32, name="idle", tag="a1")
+        for u in range(2):
+            nc.tensor.matmul_mx(
+                out=idle[:],
+                lhsT=mk_codes[:, 0:P].bitcast(FP8X4),
+                lhsT_scale=mk_sc[:, 0:P],
+                rhs=tok_codes[:].bitcast(FP8X4),
+                rhs_scale=tok_sc[:],
+                start=True,
+                stop=True,
+            )
         for g in range(3):
             nc.vector.reciprocal(out=row_inv[g][:], in_=row_sum[g][:])
         for t, part in ((0, slice(0, I)), (1, slice(0, I)), (2, slice(0, I)), (3, slice(0, I // 2)), (3, slice(I // 2, I))):
@@ -125,17 +136,6 @@ def tile_attend_externalattn_pl_kernel(tc, tok_words, tok_scales, mk, msc, mv, o
                 nc.tensor.transpose(bank[:, P * u : P * (u + 1)], col_inv[h][:, u : u + 1].to_broadcast([P, P]), ident[:])
                 spread.append(bank[:, P * u : P * (u + 1)])
 
-        idle = psum.tile([P, I], F32, name="idle", tag="b2")
-        for u in range(2):
-            nc.tensor.matmul_mx(
-                out=idle[:],
-                lhsT=mk_codes[:, 0:P].bitcast(FP8X4),
-                lhsT_scale=mk_sc[:, 0:P],
-                rhs=tok_codes[:].bitcast(FP8X4),
-                rhs_scale=tok_sc[:],
-                start=True,
-                stop=True,
-            )
         mv_b1 = keep.tile([P, PACK, P // 2, PACK], BF16, name="mv_b1", tag="neg_max3", align_bytes=64)
         deal(nc.scalar.copy, mv_b1[:], mv_raw[1][:])
         spans = [slice(CHUNK * j, CHUNK * (j + 1)) for j in range(4)]
@@ -165,6 +165,8 @@ def tile_attend_externalattn_pl_kernel(tc, tok_words, tok_scales, mk, msc, mv, o
         y_rounded = keep.tile([P, I, PACK], BF16, name="y_rounded", tag="w_b3", align_bytes=64)
         y_b = [y_rounded[:, CHUNK * j : CHUNK * (j + 1), :] for j in range(4)]
 
+        pieces = [[slice(0, CHUNK)]] * 3 + [[slice(0, CHUNK // 2), slice(CHUNK // 2, CHUNK)]]
+
         def weigh(j):
             inv = spread[j]
             nc.vector.tensor_tensor(
@@ -188,14 +190,16 @@ def tile_attend_externalattn_pl_kernel(tc, tok_words, tok_scales, mk, msc, mv, o
                     start=True,
                     stop=True,
                 )
-            nc.scalar.copy(out=y_sb[j][:], in_=bank[:])
+            for slots in pieces[j]:
+                nc.scalar.copy(out=y_sb[j][:, :, slots], in_=bank[:, :, slots])
             nc.sync.dma_start(out=out_rows[:, :, CHUNK * j : CHUNK * (j + 1)], in_=y_sb[j][:])
 
         def regroup(j):
-            nc.vector.tensor_copy(
-                out=y_b[j].rearrange("p (c n) t -> p c t n", n=4),
-                in_=y_sb[j][:].rearrange("p t (c n) -> p c t n", n=4),
-            )
+            for slots in pieces[j]:
+                nc.vector.tensor_copy(
+                    out=y_b[j][:, slots, :].rearrange("p (c n) t -> p c t n", n=4),
+                    in_=y_sb[j][:, :, slots].rearrange("p t (c n) -> p c t n", n=4),
+                )
 
         def hand_on(cols):
             nc.vector.quantize_mx(out=y_codes[:, cols].bitcast(FP8X4), scales=y_sc[:, cols], in_=y_rounded[:, cols, :].rearrange("p n t -> p (n t)"))

@@ -157,7 +157,7 @@ def tile_attend_externalattn_pl_kernel(tc, tok_words, tok_scales, mk, msc, mv, o
         y_sc = keep.tile([P, I], U8, name="y_sc", align_bytes=64)
         out_rows = out_0.rearrange("(p t) i -> p t i", t=PACK)
         out_words = out_1[0].rearrange("p n t -> p (n t)").bitcast(I32)
-        y_tags = ["a3", "b3", "b0", "b1"]
+        y_tags = [("a3",), ("b3",), ("b0",), ("b1",)]
         w_b = [keep.tile([P, CHUNK, PACK], BF16, name=f"w_b{j}", align_bytes=64) for j in range(4)]
         w_codes = [keep.tile([P, CHUNK], U32, name=f"w_codes{j}", align_bytes=64) for j in range(4)]
         w_sc = [keep.tile([P, CHUNK], U8, name=f"w_sc{j}", align_bytes=64) for j in range(4)]
@@ -167,32 +167,35 @@ def tile_attend_externalattn_pl_kernel(tc, tok_words, tok_scales, mk, msc, mv, o
 
         pieces = [[slice(0, CHUNK)]] * 3 + [[slice(0, CHUNK // 2), slice(CHUNK // 2, CHUNK)]]
 
-        def weigh(j):
-            inv = spread[j]
+        def weigh(j, slots):
+            count = (slots.stop - slots.start) // 4
             nc.vector.tensor_tensor(
-                out=w_b[j][:].rearrange("p (c n) t -> p c t n", n=4),
-                in0=sm[j].rearrange("p t (c n) -> p c t n", n=4),
-                in1=inv.rearrange("p (c n) -> p c n", n=4).unsqueeze(2).to_broadcast([P, CHUNK // 4, PACK, 4]),
+                out=w_b[j][:, slots, :].rearrange("p (c n) t -> p c t n", n=4),
+                in0=sm[j][:, :, slots].rearrange("p t (c n) -> p c t n", n=4),
+                in1=spread[j][:, slots].rearrange("p (c n) -> p c n", n=4).unsqueeze(2).to_broadcast([P, count, PACK, 4]),
                 op=ALU.mult,
             )
 
         def multiply(j):
             nc.vector.quantize_mx(out=w_codes[j][:].bitcast(FP8X4), scales=w_sc[j][:], in_=w_b[j][:].rearrange("p n t -> p (n t)"))
-            bank = psum.tile([P, PACK, CHUNK], F32, name=f"y{j}", tag=y_tags[j])
-            for t in range(PACK):
-                cols = slice(P * t, P * (t + 1))
-                nc.tensor.matmul_mx(
-                    out=bank[:, t, :],
-                    lhsT=mv_codes[:, cols].bitcast(FP8X4),
-                    lhsT_scale=mv_sc[:, cols],
-                    rhs=w_codes[j][:].bitcast(FP8X4),
-                    rhs_scale=w_sc[j][:],
-                    start=True,
-                    stop=True,
-                )
-            for slots in pieces[j]:
-                nc.scalar.copy(out=y_sb[j][:, :, slots], in_=bank[:, :, slots])
-            nc.sync.dma_start(out=out_rows[:, :, CHUNK * j : CHUNK * (j + 1)], in_=y_sb[j][:])
+            rows = PACK // len(y_tags[j])
+            for u, tag in enumerate(y_tags[j]):
+                places = slice(rows * u, rows * (u + 1))
+                bank = psum.tile([P, rows, CHUNK], F32, name=f"y{j}_{u}", tag=tag)
+                for r in range(rows):
+                    cols = slice(P * (rows * u + r), P * (rows * u + r + 1))
+                    nc.tensor.matmul_mx(
+                        out=bank[:, r, :],
+                        lhsT=mv_codes[:, cols].bitcast(FP8X4),
+                        lhsT_scale=mv_sc[:, cols],
+                        rhs=w_codes[j][:].bitcast(FP8X4),
+                        rhs_scale=w_sc[j][:],
+                        start=True,
+                        stop=True,
+                    )
+                for slots in pieces[j]:
+                    nc.scalar.copy(out=y_sb[j][:, places, slots], in_=bank[:, :, slots])
+                nc.sync.dma_start(out=out_rows[:, places, CHUNK * j : CHUNK * (j + 1)], in_=y_sb[j][:, places])
 
         def regroup(j):
             for slots in pieces[j]:
@@ -204,11 +207,12 @@ def tile_attend_externalattn_pl_kernel(tc, tok_words, tok_scales, mk, msc, mv, o
         def hand_on(cols):
             nc.vector.quantize_mx(out=y_codes[:, cols].bitcast(FP8X4), scales=y_sc[:, cols], in_=y_rounded[:, cols, :].rearrange("p n t -> p (n t)"))
 
-        weigh(0)
+        weigh(0, slice(0, CHUNK))
         quantise_mv()
         for j in range(1, 4):
-            weigh(j)
+            weigh(j, slice(0, CHUNK // 2))
             multiply(j - 1)
+            weigh(j, slice(CHUNK // 2, CHUNK))
         multiply(3)
         for j in range(4):
             regroup(j)

@@ -168,11 +168,11 @@ def tile_attend_externalattn_pl_kernel(tc, tok_words, tok_scales, mk, msc, mv, o
         pieces = [[slice(0, CHUNK)]] * 3 + [[slice(0, CHUNK // 2), slice(CHUNK // 2, CHUNK)]]
 
         def weigh(j, slots):
-            count = (slots.stop - slots.start) // 4
+            count = (slots.stop - slots.start) // 2
             nc.vector.tensor_tensor(
-                out=w_b[j][:, slots, :].rearrange("p (c n) t -> p c t n", n=4),
-                in0=sm[j][:, :, slots].rearrange("p t (c n) -> p c t n", n=4),
-                in1=spread[j][:, slots].rearrange("p (c n) -> p c n", n=4).unsqueeze(2).to_broadcast([P, count, PACK, 4]),
+                out=w_b[j][:, slots, :].rearrange("p (c n) t -> p c t n", n=2),
+                in0=sm[j][:, :, slots].rearrange("p t (c n) -> p c t n", n=2),
+                in1=spread[j][:, slots].rearrange("p (c n) -> p c n", n=2).unsqueeze(2).to_broadcast([P, count, PACK, 2]),
                 op=ALU.mult,
             )
 
@@ -200,8 +200,8 @@ def tile_attend_externalattn_pl_kernel(tc, tok_words, tok_scales, mk, msc, mv, o
         def regroup(j):
             for slots in pieces[j]:
                 nc.vector.tensor_copy(
-                    out=y_b[j][:, slots, :].rearrange("p (c n) t -> p c t n", n=4),
-                    in_=y_sb[j][:, :, slots].rearrange("p t (c n) -> p c t n", n=4),
+                    out=y_b[j][:, slots, :].rearrange("p (c n) t -> p c t n", n=2),
+                    in_=y_sb[j][:, :, slots].rearrange("p t (c n) -> p c t n", n=2),
                 )
 
         def hand_on(cols):

@@ -18,154 +18,159 @@ P = 128
 PACK = 4
 D, T, I, M, E = 512, 2048, 512, 512, 512
 CHUNK = 128
-MK_VECTOR_SHARE = 44
+CHUNKS = I // CHUNK
+HALF = E // 2
+WORDS_AHEAD = T // 4
+GATHER_PIECES = (slice(0, 256), slice(256, 384), slice(384, 512))
 FLOPS = 2 * D * M * I + 2 * M * E * I
 
 
-def deal(copy, grouped, raw):
-    copy(out=grouped.rearrange("p t s j -> p s j t"), in_=raw.rearrange("p j (s t) -> p s j t", t=PACK))
+def deal(copy, grouped, raw, places=slice(0, PACK)):
+    copy(out=grouped.rearrange("p t s j -> p s j t"), in_=raw.rearrange("p j (s t) -> p s j t", t=PACK)[:, :, :, places])
 
 
 def tile_attend_externalattn_pl_kernel(tc, tok_words, tok_scales, mk, msc, mv, offs, out_0, out_1, out_2):
     nc = tc.nc
     with ExitStack() as ctx:
         keep = ctx.enter_context(tc.tile_pool(name="keep", bufs=1))
+        turns = ctx.enter_context(tc.tile_pool(name="turns", bufs=1))
         psum = ctx.enter_context(tc.psum_pool(name="psum", bufs=1))
 
         offsets = keep.tile([P, I // 16], U16, name="offsets")
         mk_raw = keep.tile([P, PACK, M], F32, name="mk_raw", align_bytes=64)
-        pool_scales = keep.tile([P, T], U8, name="pool_scales", align_bytes=64)
         pool_words = keep.tile([P, T], I32, name="pool_words", align_bytes=64)
-        msc_cols = keep.tile([P, PACK], F32, name="msc_cols", align_bytes=64)
-        mv_raw = [keep.tile([P, PACK, E // 2], F32, name=f"mv_raw{h}", align_bytes=64) for h in range(2)]
+        tok_sc = keep.tile([P, I], U8, name="tok_sc", align_bytes=64)
+        half_bytes = PACK * HALF * 4
+        pool_scales = turns.tile([P, T], U8, name="pool_scales", align_bytes=64, offset=half_bytes - T // 2)
 
         nc.gpsimd.memset(pool_scales[:].bitcast(I32), 0)
-        nc.sync.dma_start(out=mk_raw[:], in_=mk.rearrange("(p j) m -> p j m", j=PACK))
+        nc.gpsimd.memset(tok_sc[:].bitcast(I32), 0)
+        words = tok_words[0].rearrange("p n t -> p (n t)").bitcast(I32)
+        nc.sync.dma_start(out=pool_words[:, 0:WORDS_AHEAD], in_=words[:, 0:WORDS_AHEAD])
         nc.sync.dma_start(offsets[:], offs)
-        for r in range(4):
-            nc.sync.dma_start(out=pool_scales[r:P:32, :].bitcast(I32), in_=tok_scales[0][r:16:4, :].bitcast(I32))
-        nc.sync.dma_start(out=pool_words[:], in_=tok_words[0].rearrange("p n t -> p (n t)").bitcast(I32))
-        nc.scalar.dma_start(out=msc_cols[:], in_=msc.rearrange("(p t) o -> p (t o)", t=PACK))
-        for h in range(2):
-            nc.sync.dma_start(out=mv_raw[h][:], in_=mv.rearrange("(p j) e -> p j e", j=PACK)[:, :, 256 * h : 256 * (h + 1)])
+        nc.sync.dma_start(out=pool_scales[0:P:8, :].bitcast(I32), in_=tok_scales[0].bitcast(I32))
+        nc.sync.dma_start(out=mk_raw[:], in_=mk.rearrange("(p j) m -> p j m", j=PACK))
+        nc.sync.dma_start(out=pool_words[:, WORDS_AHEAD:T], in_=words[:, WORDS_AHEAD:T])
         ident = keep.tile([P, P], F32, name="ident")
         make_identity(nc, ident[:])
 
-        mk_b = keep.tile([P, PACK, P, PACK], BF16, name="mk_b", tag="rounded_then_codes", align_bytes=64)
-        cut = MK_VECTOR_SHARE
-        deal(nc.vector.tensor_copy, mk_b[:, :, 0:cut, :], mk_raw[:, :, 0 : PACK * cut])
-        deal(nc.scalar.copy, mk_b[:, :, cut:P, :], mk_raw[:, :, PACK * cut : M])
-        tok_sc = keep.tile([P, I], U8, name="tok_sc", align_bytes=64)
-        nc.vector.tensor_copy(out=tok_sc[:], in_=pool_scales[:].indirect(offsets[:]))
-        mk_codes = keep.tile([P, M], U32, name="mk_codes", align_bytes=64)
-        mk_sc = keep.tile([P, M], U8, name="mk_sc", align_bytes=64)
-        nc.vector.quantize_mx(out=mk_codes[:].bitcast(FP8X4), scales=mk_sc[:], in_=mk_b[:].rearrange("p t s j -> p (t s j)"))
+        listed_sc = keep.tile([P, I], U8, name="listed_sc", align_bytes=64)
+        nc.vector.tensor_copy(out=listed_sc[:], in_=pool_scales[:].indirect(offsets[:]))
+        for r in range(4):
+            nc.sync.dma_start(out=tok_sc[r:P:32, :].bitcast(I32), in_=listed_sc[8 * r : P : 32, :].bitcast(I32))
+        mv_raw = [turns.tile([P, PACK, HALF], F32, name=f"mv_raw{h}", align_bytes=64, offset=half_bytes * (1 - h)) for h in range(2)]
+        for h in range(2):
+            nc.sync.dma_start(out=mv_raw[h][:], in_=mv.rearrange("(p j) e -> p j e", j=PACK)[:, :, HALF * h : HALF * (h + 1)])
+        msc_cols = keep.tile([P, PACK], F32, name="msc_cols", tag="listed_sc", align_bytes=64)
+        nc.sync.dma_start(out=msc_cols[:], in_=msc.rearrange("(p t) o -> p (t o)", t=PACK))
+
+        mk_b = [keep.tile([P, 2, P, PACK], BF16, name=f"mk_b{h}", tag=tag, align_bytes=64) for h, tag in enumerate(("rounded_then_codes", "mk_b1"))]
+        deal(nc.vector.tensor_copy, mk_b[0][:], mk_raw[:], slice(0, 2))
+        deal(nc.scalar.copy, mk_b[1][:], mk_raw[:], slice(2, 4))
+        mk_codes = [keep.tile([P, M // 2], U32, name=f"mk_codes{h}", align_bytes=64) for h in range(2)]
+        mk_sc = [keep.tile([P, M // 2], U8, name=f"mk_sc{h}", tag=tag, align_bytes=64) for h, tag in enumerate(("mk_sc0", "pool_words"))]
+
+        def quantise_mk(h):
+            nc.vector.quantize_mx(out=mk_codes[h][:].bitcast(FP8X4), scales=mk_sc[h][:], in_=mk_b[h][:].rearrange("p t s j -> p (t s j)"))
+
+        quantise_mk(0)
 
         tok_codes = keep.tile([P, I], U32, name="tok_codes", tag="rounded_then_codes", align_bytes=64)
-        for h in range(2):
+        for slots in GATHER_PIECES:
             nc.vector.tensor_copy(
-                out=tok_codes[:, 256 * h : 256 * (h + 1)],
-                in_=pool_words[:].bitcast(U32).indirect(offsets[:, 16 * h : 16 * (h + 1)]),
+                out=tok_codes[:, slots],
+                in_=pool_words[:].bitcast(U32).indirect(offsets[:, slots.start // 16 : slots.stop // 16]),
             )
+        quantise_mk(1)
 
-        mv_b0 = keep.tile([P, PACK, P // 2, PACK], BF16, name="mv_b0", align_bytes=64)
-        deal(nc.scalar.copy, mv_b0[:], mv_raw[0][:])
+        mv_b = [keep.tile([P, PACK, P // 2, PACK], BF16, name=f"mv_b{h}", tag=tag, align_bytes=64) for h, tag in enumerate(("mv_b0", "neg_max3"))]
+        deal(nc.scalar.copy, mv_b[0][:], mv_raw[0][:])
 
         scores = [psum.tile([P, I], F32, name=f"scores{t}", tag=f"a{t}") for t in range(PACK)]
         for t in range(PACK):
-            cols = slice(P * t, P * (t + 1))
-            for h in range(2):
-                slots = slice(256 * h, 256 * (h + 1))
+            cols = slice(P * (t % 2), P * (t % 2 + 1))
+            for slots in GATHER_PIECES if t == 0 else (slice(0, I),):
                 nc.tensor.matmul_mx(
                     out=scores[t][:, slots],
-                    lhsT=mk_codes[:, cols].bitcast(FP8X4),
-                    lhsT_scale=mk_sc[:, cols],
+                    lhsT=mk_codes[t // 2][:, cols].bitcast(FP8X4),
+                    lhsT_scale=mk_sc[t // 2][:, cols],
                     rhs=tok_codes[:, slots].bitcast(FP8X4),
                     rhs_scale=tok_sc[:, slots],
                     start=True,
                     stop=True,
                 )
-        p_all = keep.tile([P, PACK * I], F32, name="p_all", tag="mv_raw0", align_bytes=64)
+        p_all = turns.tile([P, PACK * I], F32, name="p_all", align_bytes=64, offset=half_bytes)
         p = [p_all[:, I * t : I * (t + 1)] for t in range(PACK)]
-        s = [keep.tile([P, I], F32, name=f"s{t}", tag=f"s{t}", align_bytes=64) for t in range(PACK)]
-        neg_max = [keep.tile([P, 1], F32, name=f"neg_max{t}", tag=f"neg_max{t}", align_bytes=64) for t in range(PACK)]
-        place = [(0, 0), (0, 1), (1, 0), (2, 0)]
-        row_sum = [keep.tile([P, n], F32, name=f"row_sum{g}", align_bytes=64) for g, n in enumerate((2, 1, 1))]
-        row_inv = [keep.tile([P, n], F32, name=f"row_inv{g}", align_bytes=64) for g, n in enumerate((2, 1, 1))]
+        s = [keep.tile([P, I], F32, name=f"s{t}", align_bytes=64) for t in range(PACK)]
+        row_groups = [[0, 1], [2], [3]]
+        sum_tiles = [keep.tile([P, len(g)], F32, name=f"row_sum{h}", align_bytes=64) for h, g in enumerate(row_groups)]
+        inv_tiles = [keep.tile([P, len(g)], F32, name=f"row_inv{h}", align_bytes=64) for h, g in enumerate(row_groups)]
+        row_sum = [sum_tiles[h][:, u : u + 1] for h, g in enumerate(row_groups) for u in range(len(g))]
+        row_inv = [inv_tiles[h][:, u : u + 1] for h, g in enumerate(row_groups) for u in range(len(g))]
+
+        def share(t, part):
+            nc.vector.tensor_scalar(out=s[t][:, part], in0=p[t][:, part], scalar1=row_inv[t], scalar2=None, op0=ALU.mult)
+
         for t in range(PACK):
-            g, c = place[t]
-            nc.vector.tensor_reduce(out=neg_max[t][:], in_=scores[t][:], axis=AX.X, op=ALU.max, negate=True)
-            nc.scalar.activation(out=p[t], in_=scores[t][:], func=ACT.Exp, bias=neg_max[t][:], scale=1.0, accum_out=row_sum[g][:, c : c + 1])
-        idle = psum.tile([P, I], F32, name="idle", tag="a1")
-        for u in range(2):
-            nc.tensor.matmul_mx(
-                out=idle[:],
-                lhsT=mk_codes[:, 0:P].bitcast(FP8X4),
-                lhsT_scale=mk_sc[:, 0:P],
-                rhs=tok_codes[:].bitcast(FP8X4),
-                rhs_scale=tok_sc[:],
-                start=True,
-                stop=True,
-            )
-        for g in range(3):
-            nc.vector.reciprocal(out=row_inv[g][:], in_=row_sum[g][:])
-        for t, part in ((0, slice(0, I)), (1, slice(0, I)), (2, slice(0, I)), (3, slice(0, I // 2)), (3, slice(I // 2, I))):
-            g, c = place[t]
-            nc.vector.tensor_scalar(out=s[t][:, part], in0=p[t][:, part], scalar1=row_inv[g][:, c : c + 1], scalar2=None, op0=ALU.mult)
+            neg_max = keep.tile([P, 1], F32, name=f"neg_max{t}", tag=f"neg_max{t}", align_bytes=64)
+            nc.vector.tensor_reduce(out=neg_max[:], in_=scores[t][:], axis=AX.X, op=ALU.max, negate=True)
+            nc.scalar.activation(out=p[t], in_=scores[t][:], func=ACT.Exp, bias=neg_max[:], scale=1.0, accum_out=row_sum[t])
+        for h in range(len(row_groups)):
+            nc.vector.reciprocal(out=inv_tiles[h][:], in_=sum_tiles[h][:])
+        for t in range(PACK - 1):
+            share(t, slice(0, I))
+        share(PACK - 1, slice(0, I // 2))
+        share(PACK - 1, slice(I // 2, I))
+
         groups = [[0], [1], [2, 3]]
         sums = [psum.tile([P, len(g), P], F32, name=f"sums{h}", tag=f"b{h}") for h, g in enumerate(groups)]
-        for h, g in enumerate(groups):
+
+        def turn(t, h):
+            g = groups[h]
+            for u, j in enumerate(g):
+                nc.tensor.matmul(
+                    out=sums[h][:, u, :],
+                    lhsT=s[t][:, P * j : P * (j + 1)],
+                    rhs=ident[:],
+                    start=(t == 0 and u == 0),
+                    stop=(t == PACK - 1 and u == len(g) - 1),
+                    is_transpose=True,
+                )
+
+        for h in range(len(groups)):
             for t in range(PACK):
-                for u, j in enumerate(g):
-                    nc.tensor.matmul(
-                        out=sums[h][:, u, :],
-                        lhsT=s[t][:, P * j : P * (j + 1)],
-                        rhs=ident[:],
-                        start=(t == 0 and u == 0),
-                        stop=(t == PACK - 1 and u == len(g) - 1),
-                        is_transpose=True,
-                    )
+                turn(t, h)
+
         col_sum = [keep.tile([P, len(g)], F32, name=f"col_sum{h}") for h, g in enumerate(groups)]
         col_inv = [keep.tile([P, len(g)], F32, name=f"col_inv{h}") for h, g in enumerate(groups)]
         spread = []
         for h, g in enumerate(groups):
             nc.vector.tensor_reduce(out=col_sum[h][:], in_=sums[h][:], axis=AX.X, op=ALU.add)
             nc.vector.reciprocal(out=col_inv[h][:], in_=col_sum[h][:])
-            bank = psum.tile([P, len(g) * P], F32, name=f"spread{h}", tag=("a0", "a1", "a2")[h])
+            bank = psum.tile([P, len(g) * P], F32, name=f"spread{h}", tag=f"a{h}")
             for u in range(len(g)):
                 nc.tensor.transpose(bank[:, P * u : P * (u + 1)], col_inv[h][:, u : u + 1].to_broadcast([P, P]), ident[:])
                 spread.append(bank[:, P * u : P * (u + 1)])
 
-        mv_b1 = keep.tile([P, PACK, P // 2, PACK], BF16, name="mv_b1", tag="neg_max3", align_bytes=64)
-        deal(nc.scalar.copy, mv_b1[:], mv_raw[1][:])
-        spans = [slice(CHUNK * j, CHUNK * (j + 1)) for j in range(4)]
-        parts = [keep.tile([P, PACK, c.stop - c.start], F32, name=f"sm{h}", tag=tag, align_bytes=64) for h, (c, tag) in enumerate(zip(spans, ("row_sum2", "neg_max2", "mv_raw1", "neg_max1")))]
-        for part, c in zip(parts, spans):
-            for t in range(PACK):
-                nc.scalar.activation(out=part[:, t, :], in_=s[t][:, c], func=ACT.Copy, scale=msc_cols[:, t : t + 1])
-        sm = [part[:] for part in parts]
-        mv_codes = keep.tile([P, E], U32, name="mv_codes", tag="mv_raw0", align_bytes=64)
+        deal(nc.scalar.copy, mv_b[1][:], mv_raw[1][:])
+        sm = [turns.tile([P, PACK, CHUNK], F32, name=f"sm{j}", align_bytes=64, offset=j * PACK * CHUNK * 4) for j in range(CHUNKS)]
+        mv_codes = turns.tile([P, E], U32, name="mv_codes", align_bytes=64, offset=2 * half_bytes)
         mv_sc = keep.tile([P, E], U8, name="mv_sc", align_bytes=64)
-
-        def quantise_mv():
-            for h, mv_b in enumerate((mv_b0, mv_b1)):
-                for t in range(PACK):
-                    cols = slice(P * t + 64 * h, P * t + 64 * (h + 1))
-                    nc.vector.quantize_mx(out=mv_codes[:, cols].bitcast(FP8X4), scales=mv_sc[:, cols], in_=mv_b[:, t].rearrange("p s j -> p (s j)"))
+        for j in range(CHUNKS):
+            for t in range(PACK):
+                nc.scalar.activation(out=sm[j][:, t, :], in_=s[t][:, CHUNK * j : CHUNK * (j + 1)], func=ACT.Copy, scale=msc_cols[:, t : t + 1])
 
         y_codes = keep.tile([P, I], U32, name="y_codes", align_bytes=64)
         y_sc = keep.tile([P, I], U8, name="y_sc", align_bytes=64)
         out_rows = out_0.rearrange("(p t) i -> p t i", t=PACK)
-        out_words = out_1[0].rearrange("p n t -> p (n t)").bitcast(I32)
-        y_tags = [("a3",), ("b3",), ("b0",), ("b1",)]
-        w_b = [keep.tile([P, CHUNK, PACK], BF16, name=f"w_b{j}", align_bytes=64) for j in range(4)]
-        w_codes = [keep.tile([P, CHUNK], U32, name=f"w_codes{j}", align_bytes=64) for j in range(4)]
-        w_sc = [keep.tile([P, CHUNK], U8, name=f"w_sc{j}", align_bytes=64) for j in range(4)]
-        y_sb = [keep.tile([P, PACK, CHUNK], F32, name=f"y_sb{j}") for j in range(4)]
+        y_tags = ("a3", "b3", "b0", "b1")
+        w_b = [keep.tile([P, CHUNK, PACK], BF16, name=f"w_b{j}", align_bytes=64) for j in range(CHUNKS)]
+        w_codes = [keep.tile([P, CHUNK], U32, name=f"w_codes{j}", align_bytes=64) for j in range(CHUNKS)]
+        w_sc = [keep.tile([P, CHUNK], U8, name=f"w_sc{j}", align_bytes=64) for j in range(CHUNKS)]
+        y_sb = [keep.tile([P, PACK, CHUNK], F32, name=f"y_sb{j}") for j in range(CHUNKS)]
         y_rounded = keep.tile([P, I, PACK], BF16, name="y_rounded", tag="w_b3", align_bytes=64)
-        y_b = [y_rounded[:, CHUNK * j : CHUNK * (j + 1), :] for j in range(4)]
-
-        pieces = [[slice(0, CHUNK)]] * 3 + [[slice(0, CHUNK // 2), slice(CHUNK // 2, CHUNK)]]
+        low, high, whole = slice(0, CHUNK // 2), slice(CHUNK // 2, CHUNK), slice(0, CHUNK)
+        pieces = [[whole]] * (CHUNKS - 1) + [[low, high]]
 
         def weigh(j, slots):
             count = (slots.stop - slots.start) // 2
@@ -178,47 +183,41 @@ def tile_attend_externalattn_pl_kernel(tc, tok_words, tok_scales, mk, msc, mv, o
 
         def multiply(j):
             nc.vector.quantize_mx(out=w_codes[j][:].bitcast(FP8X4), scales=w_sc[j][:], in_=w_b[j][:].rearrange("p n t -> p (n t)"))
-            rows = PACK // len(y_tags[j])
-            for u, tag in enumerate(y_tags[j]):
-                places = slice(rows * u, rows * (u + 1))
-                bank = psum.tile([P, rows, CHUNK], F32, name=f"y{j}_{u}", tag=tag)
-                for r in range(rows):
-                    cols = slice(P * (rows * u + r), P * (rows * u + r + 1))
-                    nc.tensor.matmul_mx(
-                        out=bank[:, r, :],
-                        lhsT=mv_codes[:, cols].bitcast(FP8X4),
-                        lhsT_scale=mv_sc[:, cols],
-                        rhs=w_codes[j][:].bitcast(FP8X4),
-                        rhs_scale=w_sc[j][:],
-                        start=True,
-                        stop=True,
-                    )
-                for slots in pieces[j]:
-                    nc.scalar.copy(out=y_sb[j][:, places, slots], in_=bank[:, :, slots])
-                nc.sync.dma_start(out=out_rows[:, places, CHUNK * j : CHUNK * (j + 1)], in_=y_sb[j][:, places])
+            bank = psum.tile([P, PACK, CHUNK], F32, name=f"y{j}", tag=y_tags[j])
+            for t in range(PACK):
+                cols = slice(P * t, P * (t + 1))
+                nc.tensor.matmul_mx(
+                    out=bank[:, t, :],
+                    lhsT=mv_codes[:, cols].bitcast(FP8X4),
+                    lhsT_scale=mv_sc[:, cols],
+                    rhs=w_codes[j][:].bitcast(FP8X4),
+                    rhs_scale=w_sc[j][:],
+                    start=True,
+                    stop=True,
+                )
+            for slots in pieces[j]:
+                nc.scalar.copy(out=y_sb[j][:, :, slots], in_=bank[:, :, slots])
+            nc.sync.dma_start(out=out_rows[:, :, CHUNK * j : CHUNK * (j + 1)], in_=y_sb[j][:])
 
-        def regroup(j):
+        weigh(0, whole)
+        for h in range(2):
+            for t in range(PACK):
+                cols = slice(P * t + 64 * h, P * t + 64 * (h + 1))
+                nc.vector.quantize_mx(out=mv_codes[:, cols].bitcast(FP8X4), scales=mv_sc[:, cols], in_=mv_b[h][:, t].rearrange("p s j -> p (s j)"))
+        for j in range(1, CHUNKS):
+            weigh(j, low)
+            multiply(j - 1)
+            weigh(j, high)
+        multiply(CHUNKS - 1)
+        for j in range(CHUNKS):
             for slots in pieces[j]:
                 nc.vector.tensor_copy(
-                    out=y_b[j][:, slots, :].rearrange("p (c n) t -> p c t n", n=2),
+                    out=y_rounded[:, CHUNK * j + slots.start : CHUNK * j + slots.stop, :].rearrange("p (c n) t -> p c t n", n=2),
                     in_=y_sb[j][:, :, slots].rearrange("p t (c n) -> p c t n", n=2),
                 )
-
-        def hand_on(cols):
-            nc.vector.quantize_mx(out=y_codes[:, cols].bitcast(FP8X4), scales=y_sc[:, cols], in_=y_rounded[:, cols, :].rearrange("p n t -> p (n t)"))
-
-        weigh(0, slice(0, CHUNK))
-        quantise_mv()
-        for j in range(1, 4):
-            weigh(j, slice(0, CHUNK // 2))
-            multiply(j - 1)
-            weigh(j, slice(CHUNK // 2, CHUNK))
-        multiply(3)
-        for j in range(4):
-            regroup(j)
         for cols in (slice(0, 256), slice(256, 384), slice(384, 512)):
-            hand_on(cols)
-        nc.sync.dma_start(out=out_words, in_=y_codes[:].bitcast(I32))
+            nc.vector.quantize_mx(out=y_codes[:, cols].bitcast(FP8X4), scales=y_sc[:, cols], in_=y_rounded[:, cols, :].rearrange("p n t -> p (n t)"))
+        nc.sync.dma_start(out=out_1[0].rearrange("p n t -> p (n t)").bitcast(I32), in_=y_codes[:].bitcast(I32))
         for q in range(4):
             queue = nc.sync if q % 2 == 0 else nc.scalar
             queue.dma_start(out=out_2[0][q:16:4, :].bitcast(I32), in_=y_sc[q:P:32, :].bitcast(I32))

@@ -20,7 +20,8 @@ D, T, I, M, E = 512, 2048, 512, 512, 512
 CHUNK = 128
 CHUNKS = I // CHUNK
 HALF = E // 2
-WORDS_AHEAD = T // 4
+WORDS_AHEAD = 3 * T // 8
+MV_PIECES = (slice(0, 128), slice(128, 256), slice(256, 320), slice(320, 512))
 GATHER_PIECES = (slice(0, 256), slice(256, 384), slice(384, 512))
 FLOPS = 2 * D * M * I + 2 * M * E * I
 
@@ -37,11 +38,11 @@ def tile_attend_externalattn_pl_kernel(tc, tok_words, tok_scales, mk, msc, mv, o
         psum = ctx.enter_context(tc.psum_pool(name="psum", bufs=1))
 
         offsets = keep.tile([P, I // 16], U16, name="offsets")
-        mk_raw = keep.tile([P, PACK, M], F32, name="mk_raw", align_bytes=64)
         pool_words = keep.tile([P, T], I32, name="pool_words", align_bytes=64)
         tok_sc = keep.tile([P, I], U8, name="tok_sc", align_bytes=64)
-        half_bytes = PACK * HALF * 4
-        pool_scales = turns.tile([P, T], U8, name="pool_scales", align_bytes=64, offset=half_bytes - T // 2)
+        row_bytes = 4 * I
+        pool_scales = turns.tile([P, T], U8, name="pool_scales", align_bytes=64, offset=row_bytes // 2)
+        mk_raw = turns.tile([P, PACK, M], F32, name="mk_raw", align_bytes=64, offset=4 * row_bytes)
 
         nc.gpsimd.memset(pool_scales[:].bitcast(I32), 0)
         nc.gpsimd.memset(tok_sc[:].bitcast(I32), 0)
@@ -58,15 +59,23 @@ def tile_attend_externalattn_pl_kernel(tc, tok_words, tok_scales, mk, msc, mv, o
         nc.vector.tensor_copy(out=listed_sc[:], in_=pool_scales[:].indirect(offsets[:]))
         for r in range(4):
             nc.sync.dma_start(out=tok_sc[r:P:32, :].bitcast(I32), in_=listed_sc[8 * r : P : 32, :].bitcast(I32))
-        mv_raw = [turns.tile([P, PACK, HALF], F32, name=f"mv_raw{h}", align_bytes=64, offset=half_bytes * (1 - h)) for h in range(2)]
-        for h in range(2):
-            nc.sync.dma_start(out=mv_raw[h][:], in_=mv.rearrange("(p j) e -> p j e", j=PACK)[:, :, HALF * h : HALF * (h + 1)])
-        msc_cols = keep.tile([P, PACK], F32, name="msc_cols", tag="listed_sc", align_bytes=64)
-        nc.sync.dma_start(out=msc_cols[:], in_=msc.rearrange("(p t) o -> p (t o)", t=PACK))
+        mv_raw = []
+
+        def load_mv(pool, **place):
+            c = MV_PIECES[len(mv_raw)]
+            raw = pool.tile([P, PACK, c.stop - c.start], F32, name=f"mv_raw{len(mv_raw)}", align_bytes=64, **place)
+            nc.sync.dma_start(out=raw[:], in_=mv.rearrange("(p j) e -> p j e", j=PACK)[:, :, c])
+            mv_raw.append(raw)
+
+        load_mv(turns, offset=0)
+        load_mv(turns, offset=row_bytes)
 
         mk_b = [keep.tile([P, 2, P, PACK], BF16, name=f"mk_b{h}", tag=tag, align_bytes=64) for h, tag in enumerate(("rounded_then_codes", "mk_b1"))]
         deal(nc.vector.tensor_copy, mk_b[0][:], mk_raw[:], slice(0, 2))
         deal(nc.scalar.copy, mk_b[1][:], mk_raw[:], slice(2, 4))
+        load_mv(turns, offset=4 * row_bytes)
+        msc_cols = keep.tile([P, PACK], F32, name="msc_cols", tag="listed_sc", align_bytes=64)
+        nc.sync.dma_start(out=msc_cols[:], in_=msc.rearrange("(p t) o -> p (t o)", t=PACK))
         mk_codes = [keep.tile([P, M // 2], U32, name=f"mk_codes{h}", align_bytes=64) for h in range(2)]
         mk_sc = [keep.tile([P, M // 2], U8, name=f"mk_sc{h}", tag=tag, align_bytes=64) for h, tag in enumerate(("mk_sc0", "pool_words"))]
 
@@ -82,9 +91,16 @@ def tile_attend_externalattn_pl_kernel(tc, tok_words, tok_scales, mk, msc, mv, o
                 in_=pool_words[:].bitcast(U32).indirect(offsets[:, slots.start // 16 : slots.stop // 16]),
             )
         quantise_mk(1)
+        load_mv(keep, tag="mk_b1")
 
-        mv_b = [keep.tile([P, PACK, P // 2, PACK], BF16, name=f"mv_b{h}", tag=tag, align_bytes=64) for h, tag in enumerate(("mv_b0", "neg_max3"))]
-        deal(nc.scalar.copy, mv_b[0][:], mv_raw[0][:])
+        mv_b = keep.tile([P, PACK, P, PACK], BF16, name="mv_b", align_bytes=64)
+
+        def cast_mv(k, copy):
+            c = MV_PIECES[k]
+            deal(copy, mv_b[:, :, c.start // PACK : c.stop // PACK, :], mv_raw[k][:])
+
+        for k in range(3):
+            cast_mv(k, nc.scalar.copy)
 
         scores = [psum.tile([P, I], F32, name=f"scores{t}", tag=f"a{t}") for t in range(PACK)]
         for t in range(PACK):
@@ -99,7 +115,7 @@ def tile_attend_externalattn_pl_kernel(tc, tok_words, tok_scales, mk, msc, mv, o
                     start=True,
                     stop=True,
                 )
-        p_all = turns.tile([P, PACK * I], F32, name="p_all", align_bytes=64, offset=half_bytes)
+        p_all = turns.tile([P, PACK * I], F32, name="p_all", align_bytes=64, offset=row_bytes)
         p = [p_all[:, I * t : I * (t + 1)] for t in range(PACK)]
         s = [keep.tile([P, I], F32, name=f"s{t}", align_bytes=64) for t in range(PACK)]
         row_groups = [[0, 1], [2], [3]]
@@ -144,19 +160,30 @@ def tile_attend_externalattn_pl_kernel(tc, tok_words, tok_scales, mk, msc, mv, o
         col_sum = [keep.tile([P, len(g)], F32, name=f"col_sum{h}") for h, g in enumerate(groups)]
         col_inv = [keep.tile([P, len(g)], F32, name=f"col_inv{h}") for h, g in enumerate(groups)]
         spread = []
-        for h, g in enumerate(groups):
-            nc.vector.tensor_reduce(out=col_sum[h][:], in_=sums[h][:], axis=AX.X, op=ALU.add)
+
+        def invert_and_spread(h):
+            g = groups[h]
             nc.vector.reciprocal(out=col_inv[h][:], in_=col_sum[h][:])
             bank = psum.tile([P, len(g) * P], F32, name=f"spread{h}", tag=f"a{h}")
             for u in range(len(g)):
                 nc.tensor.transpose(bank[:, P * u : P * (u + 1)], col_inv[h][:, u : u + 1].to_broadcast([P, P]), ident[:])
                 spread.append(bank[:, P * u : P * (u + 1)])
 
-        deal(nc.scalar.copy, mv_b[1][:], mv_raw[1][:])
-        sm = [turns.tile([P, PACK, CHUNK], F32, name=f"sm{j}", align_bytes=64, offset=j * PACK * CHUNK * 4) for j in range(CHUNKS)]
-        mv_codes = turns.tile([P, E], U32, name="mv_codes", align_bytes=64, offset=2 * half_bytes)
+        for h in (0, 1):
+            nc.vector.tensor_reduce(out=col_sum[h][:], in_=sums[h][:], axis=AX.X, op=ALU.add)
+            invert_and_spread(h)
+
+        cast_mv(3, nc.scalar.copy)
+        sm = [turns.tile([P, PACK, CHUNK], F32, name=f"sm{j}", align_bytes=64, offset=row_bytes * (j + 1)) for j in range(CHUNKS - 1)]
+        sm.append(keep.tile([P, PACK, CHUNK], F32, name="sm3", tag="neg_max3", align_bytes=64))
+        mv_codes = turns.tile([P, E], U32, name="mv_codes", align_bytes=64, offset=4 * row_bytes)
         mv_sc = keep.tile([P, E], U8, name="mv_sc", align_bytes=64)
+        summed = keep.tile([P, 2, P], F32, name="summed", align_bytes=64)
         for j in range(CHUNKS):
+            if j == 2:
+                for u in range(2):
+                    nc.scalar.activation(out=summed[:, u, :], in_=sums[2][:, u, :], func=ACT.Copy, accum_out=col_sum[2][:, u : u + 1])
+                invert_and_spread(2)
             for t in range(PACK):
                 nc.scalar.activation(out=sm[j][:, t, :], in_=s[t][:, CHUNK * j : CHUNK * (j + 1)], func=ACT.Copy, scale=msc_cols[:, t : t + 1])
 
@@ -203,7 +230,7 @@ def tile_attend_externalattn_pl_kernel(tc, tok_words, tok_scales, mk, msc, mv, o
         for h in range(2):
             for t in range(PACK):
                 cols = slice(P * t + 64 * h, P * t + 64 * (h + 1))
-                nc.vector.quantize_mx(out=mv_codes[:, cols].bitcast(FP8X4), scales=mv_sc[:, cols], in_=mv_b[h][:, t].rearrange("p s j -> p (s j)"))
+                nc.vector.quantize_mx(out=mv_codes[:, cols].bitcast(FP8X4), scales=mv_sc[:, cols], in_=mv_b[:, t, 64 * h : 64 * (h + 1), :].rearrange("p s j -> p (s j)"))
         for j in range(1, CHUNKS):
             weigh(j, low)
             multiply(j - 1)

@@ -115,6 +115,17 @@ def tile_attend_externalattn_pl_kernel(tc, tok_words, tok_scales, mk, msc, mv, o
                     start=True,
                     stop=True,
                 )
+        idle = psum.tile([P, I], F32, name="idle", tag="b3")
+        for cols in (slice(0, 256), slice(0, 128)):
+            nc.tensor.matmul_mx(
+                out=idle[:, cols],
+                lhsT=mk_codes[1][:, 0:P].bitcast(FP8X4),
+                lhsT_scale=mk_sc[1][:, 0:P],
+                rhs=mk_codes[1][:, cols].bitcast(FP8X4),
+                rhs_scale=mk_sc[1][:, cols],
+                start=True,
+                stop=True,
+            )
         p_all = turns.tile([P, PACK * I], F32, name="p_all", align_bytes=64, offset=row_bytes)
         p = [p_all[:, I * t : I * (t + 1)] for t in range(PACK)]
         s = [keep.tile([P, I], F32, name=f"s{t}", align_bytes=64) for t in range(PACK)]

@@ -115,17 +115,6 @@ def tile_attend_externalattn_pl_kernel(tc, tok_words, tok_scales, mk, msc, mv, o
                     start=True,
                     stop=True,
                 )
-        idle = psum.tile([P, I], F32, name="idle", tag="b3")
-        for cols in (slice(0, 256), slice(0, 128)):
-            nc.tensor.matmul_mx(
-                out=idle[:, cols],
-                lhsT=mk_codes[1][:, 0:P].bitcast(FP8X4),
-                lhsT_scale=mk_sc[1][:, 0:P],
-                rhs=mk_codes[1][:, cols].bitcast(FP8X4),
-                rhs_scale=mk_sc[1][:, cols],
-                start=True,
-                stop=True,
-            )
         p_all = turns.tile([P, PACK * I], F32, name="p_all", align_bytes=64, offset=row_bytes)
         p = [p_all[:, I * t : I * (t + 1)] for t in range(PACK)]
         s = [keep.tile([P, I], F32, name=f"s{t}", align_bytes=64) for t in range(PACK)]
@@ -149,6 +138,17 @@ def tile_attend_externalattn_pl_kernel(tc, tok_words, tok_scales, mk, msc, mv, o
         share(PACK - 1, slice(0, I // 2))
         share(PACK - 1, slice(I // 2, I))
 
+        idle = psum.tile([P, I], F32, name="idle", tag="a0")
+        for cols in (slice(0, 256), slice(0, 128)):
+            nc.tensor.matmul_mx(
+                out=idle[:, cols],
+                lhsT=mk_codes[1][:, 0:P].bitcast(FP8X4),
+                lhsT_scale=mk_sc[1][:, 0:P],
+                rhs=mk_codes[1][:, cols].bitcast(FP8X4),
+                rhs_scale=mk_sc[1][:, cols],
+                start=True,
+                stop=True,
+            )
         groups = [[0], [1], [2, 3]]
         sums = [psum.tile([P, len(g), P], F32, name=f"sums{h}", tag=f"b{h}") for h, g in enumerate(groups)]
 

@@ -21,8 +21,8 @@ CHUNK = 128
 CHUNKS = I // CHUNK
 HALF = E // 2
 WORDS_AHEAD = 3 * T // 8
-MV_PIECES = (slice(0, 128), slice(128, 256), slice(256, 320), slice(320, 512))
-GATHER_PIECES = (slice(0, 256), slice(256, 384), slice(384, 512))
+MV_PIECES = (slice(0, 128), slice(128, 256), slice(256, 512))
+MK_EARLY = 384
 FLOPS = 2 * D * M * I + 2 * M * E * I
 
 
@@ -42,7 +42,8 @@ def tile_attend_externalattn_pl_kernel(tc, tok_words, tok_scales, mk, msc, mv, o
         tok_sc = keep.tile([P, I], U8, name="tok_sc", align_bytes=64)
         row_bytes = 4 * I
         pool_scales = turns.tile([P, T], U8, name="pool_scales", align_bytes=64, offset=row_bytes // 2)
-        mk_raw = turns.tile([P, PACK, M], F32, name="mk_raw", align_bytes=64, offset=4 * row_bytes)
+        mk_rows = mk.rearrange("(p j) m -> p j m", j=PACK)
+        mk_early = turns.tile([P, PACK, MK_EARLY], F32, name="mk_early", align_bytes=64, offset=4 * row_bytes)
 
         nc.gpsimd.memset(pool_scales[:].bitcast(I32), 0)
         nc.gpsimd.memset(tok_sc[:].bitcast(I32), 0)
@@ -50,8 +51,10 @@ def tile_attend_externalattn_pl_kernel(tc, tok_words, tok_scales, mk, msc, mv, o
         nc.sync.dma_start(out=pool_words[:, 0:WORDS_AHEAD], in_=words[:, 0:WORDS_AHEAD])
         nc.sync.dma_start(offsets[:], offs)
         nc.sync.dma_start(out=pool_scales[0:P:8, :].bitcast(I32), in_=tok_scales[0].bitcast(I32))
-        nc.sync.dma_start(out=mk_raw[:], in_=mk.rearrange("(p j) m -> p j m", j=PACK))
         nc.sync.dma_start(out=pool_words[:, WORDS_AHEAD:T], in_=words[:, WORDS_AHEAD:T])
+        nc.sync.dma_start(out=mk_early[:], in_=mk_rows[:, :, 0:MK_EARLY])
+        mk_late = keep.tile([P, PACK, M - MK_EARLY], F32, name="mk_late", align_bytes=64)
+        nc.sync.dma_start(out=mk_late[:], in_=mk_rows[:, :, MK_EARLY:M])
         ident = keep.tile([P, P], F32, name="ident")
         make_identity(nc, ident[:])
 
@@ -69,28 +72,22 @@ def tile_attend_externalattn_pl_kernel(tc, tok_words, tok_scales, mk, msc, mv, o
 
         load_mv(turns, offset=0)
         load_mv(turns, offset=row_bytes)
+        tok_codes = keep.tile([P, I], U32, name="tok_codes", align_bytes=64)
+        nc.vector.tensor_copy(out=tok_codes[:], in_=pool_words[:].bitcast(U32).indirect(offsets[:]))
 
-        mk_b = [keep.tile([P, 2, P, PACK], BF16, name=f"mk_b{h}", tag=tag, align_bytes=64) for h, tag in enumerate(("rounded_then_codes", "mk_b1"))]
-        deal(nc.vector.tensor_copy, mk_b[0][:], mk_raw[:], slice(0, 2))
-        deal(nc.scalar.copy, mk_b[1][:], mk_raw[:], slice(2, 4))
-        load_mv(turns, offset=4 * row_bytes)
+        mk_b = [keep.tile([P, 2, P, PACK], BF16, name=f"mk_b{h}", align_bytes=64) for h in range(2)]
+        cut = MK_EARLY // PACK
+        for h, copy in enumerate((nc.vector.tensor_copy, nc.scalar.copy)):
+            deal(copy, mk_b[h][:, :, 0:cut, :], mk_early[:], slice(2 * h, 2 * h + 2))
         msc_cols = keep.tile([P, PACK], F32, name="msc_cols", tag="listed_sc", align_bytes=64)
         nc.sync.dma_start(out=msc_cols[:], in_=msc.rearrange("(p t) o -> p (t o)", t=PACK))
+        for h, copy in enumerate((nc.vector.tensor_copy, nc.scalar.copy)):
+            deal(copy, mk_b[h][:, :, cut:P, :], mk_late[:], slice(2 * h, 2 * h + 2))
         mk_codes = [keep.tile([P, M // 2], U32, name=f"mk_codes{h}", align_bytes=64) for h in range(2)]
-        mk_sc = [keep.tile([P, M // 2], U8, name=f"mk_sc{h}", tag=tag, align_bytes=64) for h, tag in enumerate(("mk_sc0", "pool_words"))]
-
-        def quantise_mk(h):
-            nc.vector.quantize_mx(out=mk_codes[h][:].bitcast(FP8X4), scales=mk_sc[h][:], in_=mk_b[h][:].rearrange("p t s j -> p (t s j)"))
-
-        quantise_mk(0)
-
-        tok_codes = keep.tile([P, I], U32, name="tok_codes", tag="rounded_then_codes", align_bytes=64)
-        for slots in GATHER_PIECES:
-            nc.vector.tensor_copy(
-                out=tok_codes[:, slots],
-                in_=pool_words[:].bitcast(U32).indirect(offsets[:, slots.start // 16 : slots.stop // 16]),
-            )
-        quantise_mk(1)
+        mk_sc = [keep.tile([P, M // 2], U8, name=f"mk_sc{h}", align_bytes=64) for h in range(2)]
+        for h, places in ((0, slice(0, 1)), (0, slice(1, 2)), (1, slice(0, 2))):
+            cols = slice(P * places.start, P * places.stop)
+            nc.vector.quantize_mx(out=mk_codes[h][:, cols].bitcast(FP8X4), scales=mk_sc[h][:, cols], in_=mk_b[h][:, places].rearrange("p t s j -> p (t s j)"))
         load_mv(keep, tag="mk_b1")
 
         mv_b = keep.tile([P, PACK, P, PACK], BF16, name="mv_b", align_bytes=64)
@@ -99,22 +96,21 @@ def tile_attend_externalattn_pl_kernel(tc, tok_words, tok_scales, mk, msc, mv, o
             c = MV_PIECES[k]
             deal(copy, mv_b[:, :, c.start // PACK : c.stop // PACK, :], mv_raw[k][:])
 
-        for k in range(3):
+        for k in range(2):
             cast_mv(k, nc.scalar.copy)
 
         scores = [psum.tile([P, I], F32, name=f"scores{t}", tag=f"a{t}") for t in range(PACK)]
         for t in range(PACK):
             cols = slice(P * (t % 2), P * (t % 2 + 1))
-            for slots in GATHER_PIECES if t == 0 else (slice(0, I),):
-                nc.tensor.matmul_mx(
-                    out=scores[t][:, slots],
-                    lhsT=mk_codes[t // 2][:, cols].bitcast(FP8X4),
-                    lhsT_scale=mk_sc[t // 2][:, cols],
-                    rhs=tok_codes[:, slots].bitcast(FP8X4),
-                    rhs_scale=tok_sc[:, slots],
-                    start=True,
-                    stop=True,
-                )
+            nc.tensor.matmul_mx(
+                out=scores[t][:],
+                lhsT=mk_codes[t // 2][:, cols].bitcast(FP8X4),
+                lhsT_scale=mk_sc[t // 2][:, cols],
+                rhs=tok_codes[:].bitcast(FP8X4),
+                rhs_scale=tok_sc[:],
+                start=True,
+                stop=True,
+            )
         p_all = turns.tile([P, PACK * I], F32, name="p_all", align_bytes=64, offset=row_bytes)
         p = [p_all[:, I * t : I * (t + 1)] for t in range(PACK)]
         s = [keep.tile([P, I], F32, name=f"s{t}", align_bytes=64) for t in range(PACK)]
@@ -184,7 +180,7 @@ def tile_attend_externalattn_pl_kernel(tc, tok_words, tok_scales, mk, msc, mv, o
             nc.vector.tensor_reduce(out=col_sum[h][:], in_=sums[h][:], axis=AX.X, op=ALU.add)
             invert_and_spread(h)
 
-        cast_mv(3, nc.scalar.copy)
+        cast_mv(2, nc.scalar.copy)
         sm = [turns.tile([P, PACK, CHUNK], F32, name=f"sm{j}", align_bytes=64, offset=row_bytes * (j + 1)) for j in range(CHUNKS - 1)]
         sm.append(keep.tile([P, PACK, CHUNK], F32, name="sm3", tag="neg_max3", align_bytes=64))
         mv_codes = turns.tile([P, E], U32, name="mv_codes", align_bytes=64, offset=4 * row_bytes)

@@ -19,7 +19,6 @@ PACK = 4
 D, T, I, M, E = 512, 2048, 512, 512, 512
 CHUNK = 128
 CHUNKS = I // CHUNK
-HALF = E // 2
 WORDS_AHEAD = 3 * T // 8
 MV_PIECES = (slice(0, 128), slice(128, 256), slice(256, 512))
 MK_EARLY = 384
@@ -145,25 +144,13 @@ def tile_attend_externalattn_pl_kernel(tc, tok_words, tok_scales, mk, msc, mv, o
                 start=True,
                 stop=True,
             )
+        sums = [psum.tile([P, P], F32, name=f"sums{j}", tag=f"b{j}") for j in range(CHUNKS)]
+        for j in range(CHUNKS):
+            order = range(PACK) if j < CHUNKS - 1 else [PACK - 1, *range(PACK - 1)]
+            for n, t in enumerate(order):
+                nc.tensor.matmul(out=sums[j][:], lhsT=s[t][:, P * j : P * (j + 1)], rhs=ident[:], start=(n == 0), stop=(n == PACK - 1), is_transpose=True)
+
         groups = [[0], [1], [2, 3]]
-        sums = [psum.tile([P, len(g), P], F32, name=f"sums{h}", tag=f"b{h}") for h, g in enumerate(groups)]
-
-        def turn(t, h):
-            g = groups[h]
-            for u, j in enumerate(g):
-                nc.tensor.matmul(
-                    out=sums[h][:, u, :],
-                    lhsT=s[t][:, P * j : P * (j + 1)],
-                    rhs=ident[:],
-                    start=(t == 0 and u == 0),
-                    stop=(t == PACK - 1 and u == len(g) - 1),
-                    is_transpose=True,
-                )
-
-        for h in range(len(groups)):
-            for t in range(PACK):
-                turn(t, h)
-
         col_sum = [keep.tile([P, len(g)], F32, name=f"col_sum{h}") for h, g in enumerate(groups)]
         col_inv = [keep.tile([P, len(g)], F32, name=f"col_inv{h}") for h, g in enumerate(groups)]
         spread = []
@@ -189,7 +176,7 @@ def tile_attend_externalattn_pl_kernel(tc, tok_words, tok_scales, mk, msc, mv, o
         for j in range(CHUNKS):
             if j == 2:
                 for u in range(2):
-                    nc.scalar.activation(out=summed[:, u, :], in_=sums[2][:, u, :], func=ACT.Copy, accum_out=col_sum[2][:, u : u + 1])
+                    nc.scalar.activation(out=summed[:, u, :], in_=sums[2 + u][:], func=ACT.Copy, accum_out=col_sum[2][:, u : u + 1])
                 invert_and_spread(2)
             for t in range(PACK):
                 nc.scalar.activation(out=sm[j][:, t, :], in_=s[t][:, CHUNK * j : CHUNK * (j + 1)], func=ACT.Copy, scale=msc_cols[:, t : t + 1])
@@ -197,14 +184,13 @@ def tile_attend_externalattn_pl_kernel(tc, tok_words, tok_scales, mk, msc, mv, o
         y_codes = keep.tile([P, I], U32, name="y_codes", align_bytes=64)
         y_sc = keep.tile([P, I], U8, name="y_sc", align_bytes=64)
         out_rows = out_0.rearrange("(p t) i -> p t i", t=PACK)
-        y_tags = ("a3", "b3", "b0", "b1")
+        y_tags = (("a3", "b0"), ("b1", "b2"), ("b3", "a0"), ("a1", "a3"))
         w_b = [keep.tile([P, CHUNK, PACK], BF16, name=f"w_b{j}", align_bytes=64) for j in range(CHUNKS)]
         w_codes = [keep.tile([P, CHUNK], U32, name=f"w_codes{j}", align_bytes=64) for j in range(CHUNKS)]
         w_sc = [keep.tile([P, CHUNK], U8, name=f"w_sc{j}", align_bytes=64) for j in range(CHUNKS)]
         y_sb = [keep.tile([P, PACK, CHUNK], F32, name=f"y_sb{j}") for j in range(CHUNKS)]
         y_rounded = keep.tile([P, I, PACK], BF16, name="y_rounded", tag="w_b3", align_bytes=64)
         low, high, whole = slice(0, CHUNK // 2), slice(CHUNK // 2, CHUNK), slice(0, CHUNK)
-        pieces = [[whole]] * (CHUNKS - 1) + [[low, high]]
 
         def weigh(j, slots):
             count = (slots.stop - slots.start) // 2
@@ -217,21 +203,30 @@ def tile_attend_externalattn_pl_kernel(tc, tok_words, tok_scales, mk, msc, mv, o
 
         def multiply(j):
             nc.vector.quantize_mx(out=w_codes[j][:].bitcast(FP8X4), scales=w_sc[j][:], in_=w_b[j][:].rearrange("p n t -> p (n t)"))
-            bank = psum.tile([P, PACK, CHUNK], F32, name=f"y{j}", tag=y_tags[j])
-            for t in range(PACK):
-                cols = slice(P * t, P * (t + 1))
-                nc.tensor.matmul_mx(
-                    out=bank[:, t, :],
-                    lhsT=mv_codes[:, cols].bitcast(FP8X4),
-                    lhsT_scale=mv_sc[:, cols],
-                    rhs=w_codes[j][:].bitcast(FP8X4),
-                    rhs_scale=w_sc[j][:],
-                    start=True,
-                    stop=True,
-                )
-            for slots in pieces[j]:
-                nc.scalar.copy(out=y_sb[j][:, :, slots], in_=bank[:, :, slots])
+            for u, tag in enumerate(y_tags[j]):
+                bank = psum.tile([P, 2, CHUNK], F32, name=f"y{j}_{u}", tag=tag)
+                for v in range(2):
+                    cols = slice(P * (2 * u + v), P * (2 * u + v + 1))
+                    nc.tensor.matmul_mx(
+                        out=bank[:, v, :],
+                        lhsT=mv_codes[:, cols].bitcast(FP8X4),
+                        lhsT_scale=mv_sc[:, cols],
+                        rhs=w_codes[j][:].bitcast(FP8X4),
+                        rhs_scale=w_sc[j][:],
+                        start=True,
+                        stop=True,
+                    )
+                nc.scalar.copy(out=y_sb[j][:, 2 * u : 2 * u + 2, :], in_=bank[:])
             nc.sync.dma_start(out=out_rows[:, :, CHUNK * j : CHUNK * (j + 1)], in_=y_sb[j][:])
+
+        def regroup(j):
+            nc.vector.tensor_copy(
+                out=y_rounded[:, CHUNK * j : CHUNK * (j + 1), :].rearrange("p (c n) t -> p c t n", n=2),
+                in_=y_sb[j][:].rearrange("p t (c n) -> p c t n", n=2),
+            )
+
+        def planes(slots):
+            nc.vector.quantize_mx(out=y_codes[:, slots].bitcast(FP8X4), scales=y_sc[:, slots], in_=y_rounded[:, slots, :].rearrange("p n t -> p (n t)"))
 
         weigh(0, whole)
         for h in range(2):
@@ -244,14 +239,14 @@ def tile_attend_externalattn_pl_kernel(tc, tok_words, tok_scales, mk, msc, mv, o
             weigh(j, high)
         multiply(CHUNKS - 1)
         for j in range(CHUNKS):
-            for slots in pieces[j]:
-                nc.vector.tensor_copy(
-                    out=y_rounded[:, CHUNK * j + slots.start : CHUNK * j + slots.stop, :].rearrange("p (c n) t -> p c t n", n=2),
-                    in_=y_sb[j][:, :, slots].rearrange("p t (c n) -> p c t n", n=2),
-                )
-        for cols in (slice(0, 256), slice(256, 384), slice(384, 512)):
-            nc.vector.quantize_mx(out=y_codes[:, cols].bitcast(FP8X4), scales=y_sc[:, cols], in_=y_rounded[:, cols, :].rearrange("p n t -> p (n t)"))
-        nc.sync.dma_start(out=out_1[0].rearrange("p n t -> p (n t)").bitcast(I32), in_=y_codes[:].bitcast(I32))
+            regroup(j)
+        words_out = out_1[0].rearrange("p n t -> p (n t)").bitcast(I32)
+        early, late = slice(0, I // 2), slice(I // 2, I)
+        planes(early)
+        nc.sync.dma_start(out=words_out[:, early], in_=y_codes[:, early].bitcast(I32))
+        for j in (2, 3):
+            planes(slice(CHUNK * j, CHUNK * (j + 1)))
+        nc.sync.dma_start(out=words_out[:, late], in_=y_codes[:, late].bitcast(I32))
         for q in range(4):
             queue = nc.sync if q % 2 == 0 else nc.scalar
             queue.dma_start(out=out_2[0][q:16:4, :].bitcast(I32), in_=y_sc[q:P:32, :].bitcast(I32))

@@ -240,13 +240,9 @@ def tile_attend_externalattn_pl_kernel(tc, tok_words, tok_scales, mk, msc, mv, o
         multiply(CHUNKS - 1)
         for j in range(CHUNKS):
             regroup(j)
-        words_out = out_1[0].rearrange("p n t -> p (n t)").bitcast(I32)
-        early, late = slice(0, I // 2), slice(I // 2, I)
-        planes(early)
-        nc.sync.dma_start(out=words_out[:, early], in_=y_codes[:, early].bitcast(I32))
-        for j in (2, 3):
-            planes(slice(CHUNK * j, CHUNK * (j + 1)))
-        nc.sync.dma_start(out=words_out[:, late], in_=y_codes[:, late].bitcast(I32))
+        for slots in (slice(0, 256), slice(256, 384), slice(384, 512)):
+            planes(slots)
+        nc.sync.dma_start(out=out_1[0].rearrange("p n t -> p (n t)").bitcast(I32), in_=y_codes[:].bitcast(I32))
         for q in range(4):
             queue = nc.sync if q % 2 == 0 else nc.scalar
             queue.dma_start(out=out_2[0][q:16:4, :].bitcast(I32), in_=y_sc[q:P:32, :].bitcast(I32))

@@ -126,12 +126,13 @@ def tile_attend_externalattn_pl_kernel(tc, tok_words, tok_scales, mk, msc, mv, o
             neg_max = keep.tile([P, 1], F32, name=f"neg_max{t}", tag=f"neg_max{t}", align_bytes=64)
             nc.vector.tensor_reduce(out=neg_max[:], in_=scores[t][:], axis=AX.X, op=ALU.max, negate=True)
             nc.scalar.activation(out=p[t], in_=scores[t][:], func=ACT.Exp, bias=neg_max[:], scale=1.0, accum_out=row_sum[t])
-        for h in range(len(row_groups)):
+        for h in range(len(row_groups) - 1):
             nc.vector.reciprocal(out=inv_tiles[h][:], in_=sum_tiles[h][:])
         for t in range(PACK - 1):
             share(t, slice(0, I))
-        share(PACK - 1, slice(0, I // 2))
-        share(PACK - 1, slice(I // 2, I))
+        nc.vector.reciprocal(out=inv_tiles[-1][:], in_=sum_tiles[-1][:])
+        share(PACK - 1, slice(0, CHUNK))
+        share(PACK - 1, slice(CHUNK, I))
 
         idle = psum.tile([P, I], F32, name="idle", tag="a0")
         for cols in (slice(0, 256), slice(0, 128)):
@@ -144,47 +145,48 @@ def tile_attend_externalattn_pl_kernel(tc, tok_words, tok_scales, mk, msc, mv, o
                 start=True,
                 stop=True,
             )
-        sums = [psum.tile([P, P], F32, name=f"sums{j}", tag=f"b{j}") for j in range(CHUNKS)]
-        for j in range(CHUNKS):
-            order = range(PACK) if j < CHUNKS - 1 else [PACK - 1, *range(PACK - 1)]
-            for n, t in enumerate(order):
-                nc.tensor.matmul(out=sums[j][:], lhsT=s[t][:, P * j : P * (j + 1)], rhs=ident[:], start=(n == 0), stop=(n == PACK - 1), is_transpose=True)
-
-        groups = [[0], [1], [2, 3]]
-        col_sum = [keep.tile([P, len(g)], F32, name=f"col_sum{h}") for h, g in enumerate(groups)]
-        col_inv = [keep.tile([P, len(g)], F32, name=f"col_inv{h}") for h, g in enumerate(groups)]
+        col_sum = [keep.tile([P, 1], F32, name=f"col_sum{j}") for j in range(CHUNKS)]
+        col_inv = [keep.tile([P, 1], F32, name=f"col_inv{j}") for j in range(CHUNKS)]
+        sums = []
         spread = []
 
-        def invert_and_spread(h):
-            g = groups[h]
-            nc.vector.reciprocal(out=col_inv[h][:], in_=col_sum[h][:])
-            bank = psum.tile([P, len(g) * P], F32, name=f"spread{h}", tag=f"a{h}")
-            for u in range(len(g)):
-                nc.tensor.transpose(bank[:, P * u : P * (u + 1)], col_inv[h][:, u : u + 1].to_broadcast([P, P]), ident[:])
-                spread.append(bank[:, P * u : P * (u + 1)])
+        def turn(j):
+            bank = psum.tile([P, P], F32, name=f"sums{j}", tag=f"b{j % 3}")
+            for t in range(PACK):
+                nc.tensor.matmul(out=bank[:], lhsT=s[t][:, P * j : P * (j + 1)], rhs=ident[:], start=(t == 0), stop=(t == PACK - 1), is_transpose=True)
+            sums.append(bank)
 
-        for h in (0, 1):
-            nc.vector.tensor_reduce(out=col_sum[h][:], in_=sums[h][:], axis=AX.X, op=ALU.add)
-            invert_and_spread(h)
+        def invert_and_spread(j):
+            nc.vector.reciprocal(out=col_inv[j][:], in_=col_sum[j][:])
+            bank = psum.tile([P, P], F32, name=f"spread{j}", tag=f"a{j}")
+            nc.tensor.transpose(bank[:], col_inv[j][:].to_broadcast([P, P]), ident[:])
+            spread.append(bank)
 
-        cast_mv(2, nc.scalar.copy)
+        for j in range(CHUNKS - 1):
+            turn(j)
+        for j in (0, 1):
+            nc.vector.tensor_reduce(out=col_sum[j][:], in_=sums[j][:], axis=AX.X, op=ALU.add)
+            invert_and_spread(j)
+        turn(CHUNKS - 1)
+
+        late = MV_PIECES[2]
+        for u in range(2):
+            deal(nc.scalar.copy, mv_b[:, 2 * u : 2 * u + 2, late.start // PACK : late.stop // PACK, :], mv_raw[2][:], slice(2 * u, 2 * u + 2))
         sm = [turns.tile([P, PACK, CHUNK], F32, name=f"sm{j}", align_bytes=64, offset=row_bytes * (j + 1)) for j in range(CHUNKS - 1)]
         sm.append(keep.tile([P, PACK, CHUNK], F32, name="sm3", tag="neg_max3", align_bytes=64))
-        mv_codes = turns.tile([P, E], U32, name="mv_codes", align_bytes=64, offset=4 * row_bytes)
+        mv_codes = keep.tile([P, E], U32, name="mv_codes", tag="neg_max1", align_bytes=64)
         mv_sc = keep.tile([P, E], U8, name="mv_sc", align_bytes=64)
         summed = keep.tile([P, 2, P], F32, name="summed", align_bytes=64)
         for j in range(CHUNKS):
-            if j == 2:
-                for u in range(2):
-                    nc.scalar.activation(out=summed[:, u, :], in_=sums[2 + u][:], func=ACT.Copy, accum_out=col_sum[2][:, u : u + 1])
-                invert_and_spread(2)
+            if j >= 2:
+                nc.scalar.activation(out=summed[:, j - 2, :], in_=sums[j][:], func=ACT.Copy, accum_out=col_sum[j][:])
             for t in range(PACK):
                 nc.scalar.activation(out=sm[j][:, t, :], in_=s[t][:, CHUNK * j : CHUNK * (j + 1)], func=ACT.Copy, scale=msc_cols[:, t : t + 1])
 
         y_codes = keep.tile([P, I], U32, name="y_codes", align_bytes=64)
         y_sc = keep.tile([P, I], U8, name="y_sc", align_bytes=64)
         out_rows = out_0.rearrange("(p t) i -> p t i", t=PACK)
-        y_tags = (("a3", "b0"), ("b1", "b2"), ("b3", "a0"), ("a1", "a3"))
+        y_tags = (("b3", "b1"), ("b2", "b0"), ("a0", "a1"), ("b3", "b1"))
         w_b = [keep.tile([P, CHUNK, PACK], BF16, name=f"w_b{j}", align_bytes=64) for j in range(CHUNKS)]
         w_codes = [keep.tile([P, CHUNK], U32, name=f"w_codes{j}", align_bytes=64) for j in range(CHUNKS)]
         w_sc = [keep.tile([P, CHUNK], U8, name=f"w_sc{j}", align_bytes=64) for j in range(CHUNKS)]
@@ -229,6 +231,7 @@ def tile_attend_externalattn_pl_kernel(tc, tok_words, tok_scales, mk, msc, mv, o
             nc.vector.quantize_mx(out=y_codes[:, slots].bitcast(FP8X4), scales=y_sc[:, slots], in_=y_rounded[:, slots, :].rearrange("p n t -> p (n t)"))
 
         weigh(0, whole)
+        invert_and_spread(2)
         for h in range(2):
             for t in range(PACK):
                 cols = slice(P * t + 64 * h, P * t + 64 * (h + 1))
@@ -236,6 +239,8 @@ def tile_attend_externalattn_pl_kernel(tc, tok_words, tok_scales, mk, msc, mv, o
         for j in range(1, CHUNKS):
             weigh(j, low)
             multiply(j - 1)
+            if j == 1:
+                invert_and_spread(3)
             weigh(j, high)
         multiply(CHUNKS - 1)
         for j in range(CHUNKS):

@@ -152,8 +152,9 @@ def tile_attend_externalattn_pl_kernel(tc, tok_words, tok_scales, mk, msc, mv, o
 
         def turn(j):
             bank = psum.tile([P, P], F32, name=f"sums{j}", tag=f"b{j % 3}")
-            for t in range(PACK):
-                nc.tensor.matmul(out=bank[:], lhsT=s[t][:, P * j : P * (j + 1)], rhs=ident[:], start=(t == 0), stop=(t == PACK - 1), is_transpose=True)
+            order = (0, 3, 1, 2) if j == 2 else range(PACK)
+            for n, t in enumerate(order):
+                nc.tensor.matmul(out=bank[:], lhsT=s[t][:, P * j : P * (j + 1)], rhs=ident[:], start=(n == 0), stop=(n == PACK - 1), is_transpose=True)
             sums.append(bank)
 
         def invert_and_spread(j):
@@ -172,16 +173,27 @@ def tile_attend_externalattn_pl_kernel(tc, tok_words, tok_scales, mk, msc, mv, o
         late = MV_PIECES[2]
         for u in range(2):
             deal(nc.scalar.copy, mv_b[:, 2 * u : 2 * u + 2, late.start // PACK : late.stop // PACK, :], mv_raw[2][:], slice(2 * u, 2 * u + 2))
-        sm = [turns.tile([P, PACK, CHUNK], F32, name=f"sm{j}", align_bytes=64, offset=row_bytes * (j + 1)) for j in range(CHUNKS - 1)]
-        sm.append(keep.tile([P, PACK, CHUNK], F32, name="sm3", tag="neg_max3", align_bytes=64))
+        sm_first = turns.tile([P, PACK, 2 * CHUNK], F32, name="sm_first", align_bytes=64, offset=row_bytes)
+        sm_third = turns.tile([P, PACK, CHUNK], F32, name="sm_third", align_bytes=64, offset=3 * row_bytes)
+        sm_last = keep.tile([P, PACK, CHUNK], F32, name="sm_last", tag="neg_max3", align_bytes=64)
+        sm = [sm_first[:, :, 0:CHUNK], sm_first[:, :, CHUNK : 2 * CHUNK], sm_third[:], sm_last[:]]
         mv_codes = keep.tile([P, E], U32, name="mv_codes", tag="neg_max1", align_bytes=64)
         mv_sc = keep.tile([P, E], U8, name="mv_sc", align_bytes=64)
         summed = keep.tile([P, 2, P], F32, name="summed", align_bytes=64)
-        for j in range(CHUNKS):
-            if j >= 2:
-                nc.scalar.activation(out=summed[:, j - 2, :], in_=sums[j][:], func=ACT.Copy, accum_out=col_sum[j][:])
-            for t in range(PACK):
-                nc.scalar.activation(out=sm[j][:, t, :], in_=s[t][:, CHUNK * j : CHUNK * (j + 1)], func=ACT.Copy, scale=msc_cols[:, t : t + 1])
+
+        def scale_by_key(out, slots, places=range(PACK)):
+            for t in places:
+                nc.scalar.activation(out=out[:, t, :], in_=s[t][:, slots], func=ACT.Copy, scale=msc_cols[:, t : t + 1])
+
+        def sum_columns(j):
+            nc.scalar.activation(out=summed[:, j - 2, :], in_=sums[j][:], func=ACT.Copy, accum_out=col_sum[j][:])
+
+        scale_by_key(sm_first, slice(0, 2 * CHUNK))
+        sum_columns(2)
+        scale_by_key(sm_third, slice(2 * CHUNK, 3 * CHUNK), (0, 1))
+        sum_columns(3)
+        scale_by_key(sm_third, slice(2 * CHUNK, 3 * CHUNK), (2, 3))
+        scale_by_key(sm_last, slice(3 * CHUNK, I))
 
         y_codes = keep.tile([P, I], U32, name="y_codes", align_bytes=64)
         y_sc = keep.tile([P, I], U8, name="y_sc", align_bytes=64)
@@ -238,9 +250,9 @@ def tile_attend_externalattn_pl_kernel(tc, tok_words, tok_scales, mk, msc, mv, o
                 nc.vector.quantize_mx(out=mv_codes[:, cols].bitcast(FP8X4), scales=mv_sc[:, cols], in_=mv_b[:, t, 64 * h : 64 * (h + 1), :].rearrange("p s j -> p (s j)"))
         for j in range(1, CHUNKS):
             weigh(j, low)
-            multiply(j - 1)
             if j == 1:
                 invert_and_spread(3)
+            multiply(j - 1)
             weigh(j, high)
         multiply(CHUNKS - 1)
         for j in range(CHUNKS):

from contextlib import ExitStack

import concourse.mybir as mybir
from concourse.masks import make_identity

F32 = mybir.dt.float32
BF16 = mybir.dt.bfloat16
I32 = mybir.dt.int32
U32 = mybir.dt.uint32
U16 = mybir.dt.uint16
U8 = mybir.dt.uint8
FP8X4 = mybir.dt.float8_e4m3fn_x4
ACT = mybir.ActivationFunctionType
ALU = mybir.AluOpType
AX = mybir.AxisListType

P = 128
PACK = 4
D, T, I, M, E = 512, 2048, 512, 512, 512
CHUNK = 128
CHUNKS = I // CHUNK
WORDS_AHEAD = 3 * T // 8
MV_PIECES = (slice(0, 128), slice(128, 256), slice(256, 512))
MK_EARLY = 384
FLOPS = 2 * D * M * I + 2 * M * E * I


def deal(copy, grouped, raw, places=slice(0, PACK)):
    copy(out=grouped.rearrange("p t s j -> p s j t"), in_=raw.rearrange("p j (s t) -> p s j t", t=PACK)[:, :, :, places])


def tile_attend_externalattn_pl_kernel(tc, tok_words, tok_scales, mk, msc, mv, offs, out_0, out_1, out_2):
    nc = tc.nc
    with ExitStack() as ctx:
        keep = ctx.enter_context(tc.tile_pool(name="keep", bufs=1))
        turns = ctx.enter_context(tc.tile_pool(name="turns", bufs=1))
        psum = ctx.enter_context(tc.psum_pool(name="psum", bufs=1))

        offsets = keep.tile([P, I // 16], U16, name="offsets")
        pool_words = keep.tile([P, T], I32, name="pool_words", align_bytes=64)
        tok_sc = keep.tile([P, I], U8, name="tok_sc", align_bytes=64)
        row_bytes = 4 * I
        pool_scales = turns.tile([P, T], U8, name="pool_scales", align_bytes=64, offset=row_bytes // 2)
        mk_rows = mk.rearrange("(p j) m -> p j m", j=PACK)
        mk_early = turns.tile([P, PACK, MK_EARLY], F32, name="mk_early", align_bytes=64, offset=4 * row_bytes)

        nc.gpsimd.memset(pool_scales[:].bitcast(I32), 0)
        nc.gpsimd.memset(tok_sc[:].bitcast(I32), 0)
        words = tok_words[0].rearrange("p n t -> p (n t)").bitcast(I32)
        nc.sync.dma_start(out=pool_words[:, 0:WORDS_AHEAD], in_=words[:, 0:WORDS_AHEAD])
        nc.sync.dma_start(offsets[:], offs)
        nc.sync.dma_start(out=pool_scales[0:P:8, :].bitcast(I32), in_=tok_scales[0].bitcast(I32))
        nc.sync.dma_start(out=pool_words[:, WORDS_AHEAD:T], in_=words[:, WORDS_AHEAD:T])
        nc.sync.dma_start(out=mk_early[:], in_=mk_rows[:, :, 0:MK_EARLY])
        mk_late = keep.tile([P, PACK, M - MK_EARLY], F32, name="mk_late", align_bytes=64)
        nc.sync.dma_start(out=mk_late[:], in_=mk_rows[:, :, MK_EARLY:M])
        ident = keep.tile([P, P], F32, name="ident")
        make_identity(nc, ident[:])

        listed_sc = keep.tile([P, I], U8, name="listed_sc", align_bytes=64)
        nc.vector.tensor_copy(out=listed_sc[:], in_=pool_scales[:].indirect(offsets[:]))
        for r in range(4):
            nc.sync.dma_start(out=tok_sc[r:P:32, :].bitcast(I32), in_=listed_sc[8 * r : P : 32, :].bitcast(I32))
        mv_raw = []

        def load_mv(pool, **place):
            c = MV_PIECES[len(mv_raw)]
            raw = pool.tile([P, PACK, c.stop - c.start], F32, name=f"mv_raw{len(mv_raw)}", align_bytes=64, **place)
            nc.sync.dma_start(out=raw[:], in_=mv.rearrange("(p j) e -> p j e", j=PACK)[:, :, c])
            mv_raw.append(raw)

        load_mv(turns, offset=0)
        load_mv(turns, offset=row_bytes)
        tok_codes = keep.tile([P, I], U32, name="tok_codes", align_bytes=64)
        nc.vector.tensor_copy(out=tok_codes[:], in_=pool_words[:].bitcast(U32).indirect(offsets[:]))

        mk_b = [keep.tile([P, 2, P, PACK], BF16, name=f"mk_b{h}", align_bytes=64) for h in range(2)]
        cut = MK_EARLY // PACK
        for h, copy in enumerate((nc.vector.tensor_copy, nc.scalar.copy)):
            deal(copy, mk_b[h][:, :, 0:cut, :], mk_early[:], slice(2 * h, 2 * h + 2))
        msc_cols = keep.tile([P, PACK], F32, name="msc_cols", tag="listed_sc", align_bytes=64)
        nc.sync.dma_start(out=msc_cols[:], in_=msc.rearrange("(p t) o -> p (t o)", t=PACK))
        for h, copy in enumerate((nc.vector.tensor_copy, nc.scalar.copy)):
            deal(copy, mk_b[h][:, :, cut:P, :], mk_late[:], slice(2 * h, 2 * h + 2))
        mk_codes = [keep.tile([P, M // 2], U32, name=f"mk_codes{h}", align_bytes=64) for h in range(2)]
        mk_sc = [keep.tile([P, M // 2], U8, name=f"mk_sc{h}", align_bytes=64) for h in range(2)]
        for h, places in ((0, slice(0, 1)), (0, slice(1, 2)), (1, slice(0, 2))):
            cols = slice(P * places.start, P * places.stop)
            nc.vector.quantize_mx(out=mk_codes[h][:, cols].bitcast(FP8X4), scales=mk_sc[h][:, cols], in_=mk_b[h][:, places].rearrange("p t s j -> p (t s j)"))
        load_mv(keep, tag="mk_b1")

        mv_b = keep.tile([P, PACK, P, PACK], BF16, name="mv_b", align_bytes=64)

        def cast_mv(k, copy):
            c = MV_PIECES[k]
            deal(copy, mv_b[:, :, c.start // PACK : c.stop // PACK, :], mv_raw[k][:])

        for k in range(2):
            cast_mv(k, nc.scalar.copy)

        scores = [psum.tile([P, I], F32, name=f"scores{t}", tag=f"a{t}") for t in range(PACK)]
        for t in range(PACK):
            cols = slice(P * (t % 2), P * (t % 2 + 1))
            nc.tensor.matmul_mx(
                out=scores[t][:],
                lhsT=mk_codes[t // 2][:, cols].bitcast(FP8X4),
                lhsT_scale=mk_sc[t // 2][:, cols],
                rhs=tok_codes[:].bitcast(FP8X4),
                rhs_scale=tok_sc[:],
                start=True,
                stop=True,
            )
        p_all = turns.tile([P, PACK * I], F32, name="p_all", align_bytes=64, offset=row_bytes)
        p = [p_all[:, I * t : I * (t + 1)] for t in range(PACK)]
        s = [keep.tile([P, I], F32, name=f"s{t}", align_bytes=64) for t in range(PACK)]
        row_groups = [[0, 1], [2], [3]]
        sum_tiles = [keep.tile([P, len(g)], F32, name=f"row_sum{h}", align_bytes=64) for h, g in enumerate(row_groups)]
        inv_tiles = [keep.tile([P, len(g)], F32, name=f"row_inv{h}", align_bytes=64) for h, g in enumerate(row_groups)]
        row_sum = [sum_tiles[h][:, u : u + 1] for h, g in enumerate(row_groups) for u in range(len(g))]
        row_inv = [inv_tiles[h][:, u : u + 1] for h, g in enumerate(row_groups) for u in range(len(g))]

        def share(t, part):
            nc.vector.tensor_scalar(out=s[t][:, part], in0=p[t][:, part], scalar1=row_inv[t], scalar2=None, op0=ALU.mult)

        for t in range(PACK):
            neg_max = keep.tile([P, 1], F32, name=f"neg_max{t}", tag=f"neg_max{t}", align_bytes=64)
            nc.vector.tensor_reduce(out=neg_max[:], in_=scores[t][:], axis=AX.X, op=ALU.max, negate=True)
            nc.scalar.activation(out=p[t], in_=scores[t][:], func=ACT.Exp, bias=neg_max[:], scale=1.0, accum_out=row_sum[t])
        for h in range(len(row_groups) - 1):
            nc.vector.reciprocal(out=inv_tiles[h][:], in_=sum_tiles[h][:])
        for t in range(PACK - 1):
            share(t, slice(0, I))
        nc.vector.reciprocal(out=inv_tiles[-1][:], in_=sum_tiles[-1][:])
        share(PACK - 1, slice(0, CHUNK))
        share(PACK - 1, slice(CHUNK, I))

        idle = psum.tile([P, I], F32, name="idle", tag="a0")
        for cols in (slice(0, 256), slice(0, 128)):
            nc.tensor.matmul_mx(
                out=idle[:, cols],
                lhsT=mk_codes[1][:, 0:P].bitcast(FP8X4),
                lhsT_scale=mk_sc[1][:, 0:P],
                rhs=mk_codes[1][:, cols].bitcast(FP8X4),
                rhs_scale=mk_sc[1][:, cols],
                start=True,
                stop=True,
            )
        col_sum = [keep.tile([P, 1], F32, name=f"col_sum{j}") for j in range(CHUNKS)]
        col_inv = [keep.tile([P, 1], F32, name=f"col_inv{j}") for j in range(CHUNKS)]
        sums = []
        spread = []

        def turn(j):
            bank = psum.tile([P, P], F32, name=f"sums{j}", tag=f"b{j % 3}")
            order = (0, 3, 1, 2) if j == 2 else range(PACK)
            for n, t in enumerate(order):
                nc.tensor.matmul(out=bank[:], lhsT=s[t][:, P * j : P * (j + 1)], rhs=ident[:], start=(n == 0), stop=(n == PACK - 1), is_transpose=True)
            sums.append(bank)

        def invert_and_spread(j):
            nc.vector.reciprocal(out=col_inv[j][:], in_=col_sum[j][:])
            bank = psum.tile([P, P], F32, name=f"spread{j}", tag=f"a{j}")
            nc.tensor.transpose(bank[:], col_inv[j][:].to_broadcast([P, P]), ident[:])
            spread.append(bank)

        for j in range(CHUNKS - 1):
            turn(j)
        for j in (0, 1):
            nc.vector.tensor_reduce(out=col_sum[j][:], in_=sums[j][:], axis=AX.X, op=ALU.add)
            invert_and_spread(j)
        turn(CHUNKS - 1)

        late = MV_PIECES[2]
        for u in range(2):
            deal(nc.scalar.copy, mv_b[:, 2 * u : 2 * u + 2, late.start // PACK : late.stop // PACK, :], mv_raw[2][:], slice(2 * u, 2 * u + 2))
        sm_first = turns.tile([P, PACK, 2 * CHUNK], F32, name="sm_first", align_bytes=64, offset=row_bytes)
        sm_third = turns.tile([P, PACK, CHUNK], F32, name="sm_third", align_bytes=64, offset=3 * row_bytes)
        sm_last = keep.tile([P, PACK, CHUNK], F32, name="sm_last", tag="neg_max3", align_bytes=64)
        sm = [sm_first[:, :, 0:CHUNK], sm_first[:, :, CHUNK : 2 * CHUNK], sm_third[:], sm_last[:]]
        mv_codes = keep.tile([P, E], U32, name="mv_codes", tag="neg_max1", align_bytes=64)
        mv_sc = keep.tile([P, E], U8, name="mv_sc", align_bytes=64)
        summed = keep.tile([P, 2, P], F32, name="summed", align_bytes=64)

        def scale_by_key(out, slots, places=range(PACK)):
            for t in places:
                nc.scalar.activation(out=out[:, t, :], in_=s[t][:, slots], func=ACT.Copy, scale=msc_cols[:, t : t + 1])

        def sum_columns(j):
            nc.scalar.activation(out=summed[:, j - 2, :], in_=sums[j][:], func=ACT.Copy, accum_out=col_sum[j][:])

        scale_by_key(sm_first, slice(0, 2 * CHUNK))
        sum_columns(2)
        scale_by_key(sm_third, slice(2 * CHUNK, 3 * CHUNK), (0, 1))
        sum_columns(3)
        scale_by_key(sm_third, slice(2 * CHUNK, 3 * CHUNK), (2, 3))
        scale_by_key(sm_last, slice(3 * CHUNK, I))

        y_codes = keep.tile([P, I], U32, name="y_codes", align_bytes=64)
        y_sc = keep.tile([P, I], U8, name="y_sc", align_bytes=64)
        out_rows = out_0.rearrange("(p t) i -> p t i", t=PACK)
        y_tags = (("b3", "b1"), ("b2", "b0"), ("a0", "a1"), ("b3", "b1"))
        w_b = [keep.tile([P, CHUNK, PACK], BF16, name=f"w_b{j}", align_bytes=64) for j in range(CHUNKS)]
        w_codes = [keep.tile([P, CHUNK], U32, name=f"w_codes{j}", align_bytes=64) for j in range(CHUNKS)]
        w_sc = [keep.tile([P, CHUNK], U8, name=f"w_sc{j}", align_bytes=64) for j in range(CHUNKS)]
        y_sb = [keep.tile([P, PACK, CHUNK], F32, name=f"y_sb{j}") for j in range(CHUNKS)]
        y_rounded = keep.tile([P, I, PACK], BF16, name="y_rounded", tag="w_b3", align_bytes=64)
        low, high, whole = slice(0, CHUNK // 2), slice(CHUNK // 2, CHUNK), slice(0, CHUNK)

        def weigh(j, slots):
            count = (slots.stop - slots.start) // 2
            nc.vector.tensor_tensor(
                out=w_b[j][:, slots, :].rearrange("p (c n) t -> p c t n", n=2),
                in0=sm[j][:, :, slots].rearrange("p t (c n) -> p c t n", n=2),
                in1=spread[j][:, slots].rearrange("p (c n) -> p c n", n=2).unsqueeze(2).to_broadcast([P, count, PACK, 2]),
                op=ALU.mult,
            )

        def multiply(j):
            nc.vector.quantize_mx(out=w_codes[j][:].bitcast(FP8X4), scales=w_sc[j][:], in_=w_b[j][:].rearrange("p n t -> p (n t)"))
            for u, tag in enumerate(y_tags[j]):
                bank = psum.tile([P, 2, CHUNK], F32, name=f"y{j}_{u}", tag=tag)
                for v in range(2):
                    cols = slice(P * (2 * u + v), P * (2 * u + v + 1))
                    nc.tensor.matmul_mx(
                        out=bank[:, v, :],
                        lhsT=mv_codes[:, cols].bitcast(FP8X4),
                        lhsT_scale=mv_sc[:, cols],
                        rhs=w_codes[j][:].bitcast(FP8X4),
                        rhs_scale=w_sc[j][:],
                        start=True,
                        stop=True,
                    )
                nc.scalar.copy(out=y_sb[j][:, 2 * u : 2 * u + 2, :], in_=bank[:])
            nc.sync.dma_start(out=out_rows[:, :, CHUNK * j : CHUNK * (j + 1)], in_=y_sb[j][:])

        def regroup(j):
            nc.vector.tensor_copy(
                out=y_rounded[:, CHUNK * j : CHUNK * (j + 1), :].rearrange("p (c n) t -> p c t n", n=2),
                in_=y_sb[j][:].rearrange("p t (c n) -> p c t n", n=2),
            )

        def planes(slots):
            nc.vector.quantize_mx(out=y_codes[:, slots].bitcast(FP8X4), scales=y_sc[:, slots], in_=y_rounded[:, slots, :].rearrange("p n t -> p (n t)"))

        weigh(0, whole)
        invert_and_spread(2)
        for h in range(2):
            for t in range(PACK):
                cols = slice(P * t + 64 * h, P * t + 64 * (h + 1))
                nc.vector.quantize_mx(out=mv_codes[:, cols].bitcast(FP8X4), scales=mv_sc[:, cols], in_=mv_b[:, t, 64 * h : 64 * (h + 1), :].rearrange("p s j -> p (s j)"))
        for j in range(1, CHUNKS):
            weigh(j, low)
            if j == 1:
                invert_and_spread(3)
            multiply(j - 1)
            weigh(j, high)
        multiply(CHUNKS - 1)
        for j in range(CHUNKS):
            regroup(j)
        for slots in (slice(0, 256), slice(256, 384), slice(384, 512)):
            planes(slots)
        nc.sync.dma_start(out=out_1[0].rearrange("p n t -> p (n t)").bitcast(I32), in_=y_codes[:].bitcast(I32))
        for q in range(4):
            queue = nc.sync if q % 2 == 0 else nc.scalar
            queue.dma_start(out=out_2[0][q:16:4, :].bitcast(I32), in_=y_sc[q:P:32, :].bitcast(I32))
